import numpy as np, ml_dtypes
CORES = [16,17,18,19,150,151]
N = 6
BF = ml_dtypes.bfloat16
W, P, RO, L = 1408, 1, 5, 256
Q = 1.0
def parts(rng):
    share = rng.choice(np.array([0.015, 0.025, 0.04]), (N, 8, 1, 1)) * Q
    r = np.where(rng.random((N, 8, 16, W)) < share, rng.integers(5, 16, (N, 8, 16, W)), rng.integers(0, 5, (N, 8, 16, W)))
    hot = (rng.random((N, 8, 1, W)) < 0.004 * Q) & (rng.random((N, 8, 16, W)) < 0.7)
    r = np.where(hot, 15, r)
    return r, rng.integers(0, 256, (N, 8, 16, W)), rng.integers(0, W, (N, 8, 16, W)), rng.integers(0, W, (N, 8, 16, L))
def pack(r, x, k, s):
    return {"rec": np.ascontiguousarray(r.reshape(N, 128, W)).astype(np.float32).astype(BF), "wealth": np.ascontiguousarray(x.reshape(N, 128, W)).astype(np.float32).astype(BF),
            "kin": np.ascontiguousarray(k.reshape(N, 128, W)).astype(np.int32), "slips": np.ascontiguousarray(s.reshape(N, 128, L)).astype(np.int32)}
def setup_inputs(rng):
    r, x, k, s = parts(rng)
    return pack(r, x, k, s)
def setup_inputs_spread(rng):
    e = np.exp2(4.3 + 3.9 * rng.random((N, 8, 16, 1))) / Q
    r = np.minimum((16 * rng.random((N, 8, 16, W)) ** e).astype(np.int64), 15)
    x = np.minimum((np.exp2(8 * rng.random((N, 8, 1, W))) * rng.random((N, 8, 16, W))).astype(np.int64), 255)
    k = np.minimum((W * rng.random((N, 8, 16, W)) ** 2).astype(np.int64), W - 1)
    s = np.minimum((W * rng.random((N, 8, 16, L)) ** (1 + rng.random((N, 8, 1, L)))).astype(np.int64), W - 1)
    return pack(r, x, k, s)
def setup_inputs_ends(rng):
    r = 15 * (rng.random((N, 8, 16, W)) < 0.02 * Q)
    r = np.where(rng.random((N, 8, 1, W)) < 0.004 * Q, 15, r)
    w = rng.random((N, 8, 1, W)); x = 255 * np.where(w < 0.4, 0, np.where(w < 0.7, 1, rng.integers(0, 2, (N, 8, 16, W))))
    u = rng.random((N, 8, 16, W))
    k = np.where(u < 0.36, 0, np.where(u < 0.72, W - 1, np.where(u < 0.78, W - 2, rng.integers(0, W, (N, 8, 16, W)))))
    for first, places in ((1, ((2, W - 2), (15, W - 1))), (3, ((4, W - 1), (9, 5), (12, 5))), (6, ((4, 5), (9, W - 1)))):
        c = np.zeros((16, 1), np.int64)
        for m, v in places: c[m, 0] = v
        k[:, :, :, first::8] = c; x[:, :, :, first::8] = 0
    m = (np.arange(W) & 4) == 4
    k[:, 7] = np.where(m & (k[:, 7] == W - 1), 0, k[:, 7])
    a, b = W - 600, W - 344
    k[:, :, :, a:b] = 0; r[:, :, :, a:b] = 0; x[:, :, :, a:b] = 0
    k[:, :, :, W - 40:W - 24] = 0; r[:, :, :, W - 40:W - 24] = 0; x[:, :, :, W - 40:W - 24] = 0; k[:, :, 15, W - 32:W - 24] = W - 1
    r[:, :, :, 0] = 0; r[:, :, :, W - 1] = 15 * (rng.random((N, 8, 16)) < rng.choice(np.array([0.05, 0.15, 0.3]), (N, 8, 1))); r[:, 7, :, W - 1] = 15
    r[:, :, :, W - 2] = 0; r[:, :, :, 5] = 0
    x[:, :, :, 0] = 0; x[:, :, :, W - 1] = 255; x[:, :, :, 5] = 255; x[:, :, :, W - 2] = 255; x[:, :, 15, W - 2] = 254
    u = rng.random((N, 8, 16, L)); s = np.where(u < 0.35, 0, np.where(u < 0.7, W - 1, rng.integers(1, W - 600, (N, 8, 16, L))))
    s[:, :, :, 112:128] = W - 1
    for q in range(2):
        for g in range(8): s[q, g, :, 240:] = a + rng.permutation(256).reshape(16, 16)
    p = np.arange(16); s[N - 1, 7, :, 255] = np.where((p & 1) == 0, W - 40 + (p >> 1), W - 32 + (p >> 1))
    return pack(r, x, k, s)
def setup_inputs_corners(rng):
    r, x, k, s = parts(rng); own = np.arange(W); lane = np.arange(L)
    k[:, :4] = own
    n = rng.choice(np.array([0, 1, 3, 7, 8, 9, 11, 12, 13, 16]), (1, 4, 1, W)); order = np.argsort(rng.random((1, 4, 16, W)), axis=2)
    high = np.where(rng.random((N, 4, 16, W)) < 0.7, 15, rng.integers(6, 16, (N, 4, 16, W)))
    low = np.where(rng.random((N, 4, 16, W)) < 0.15, 5, rng.integers(0, 5, (N, 4, 16, W)))
    high[:, 1] = 6; low[:, 1] = 5; high[:, 2] = 6 + (own & 7); low[:, 2] = 5 + (own & 7)
    r[:, :4] = np.where(order < n, high, low)
    s[:, :2] = lane + 256 * rng.integers(0, W // 256, (N, 2, 16, L))
    s[:, 4] = np.repeat(rng.integers(0, W, (N, 1, 16)), 16, axis=2)
    for q in range(N):
        if (q & 1) == 0: s[q, 5] = rng.integers(0, W)
        else: s[q, 5] = lane + 256 * rng.integers(0, W // 256, (16, L))
    k[:, 6] = rng.choice(np.array([0, W - 1, W // 2]), (N, 1, W))
    z = rng.integers(0, 3, (N, 16, W)); k[:, 7] = np.where(z == 0, 0, np.where(z == 1, W - 1, own))
    r[:, 6:, :, [0, W - 1, W // 2]] = np.where(rng.random((N, 2, 16, 3)) < 0.2, 15, rng.integers(0, 5, (N, 2, 16, 3)))
    s[:, 7] = np.where(rng.random((N, 16, L)) < 0.1, rng.choice(np.array([0, W - 1]), (N, 16, L)), s[:, 7])
    x[:, 1] = 255; x[:, 2] = 255 * rng.integers(0, 2, (N, 1, W))
    return pack(r, x, k, s)
def setup_inputs_alike(rng):
    r, x, k, s = parts(rng)
    pool = np.repeat(rng.integers(0, W, (N, 8, 16, 6)), 16, axis=2)
    few = np.take_along_axis(pool, rng.integers(0, 6, (N, 8, L, 16)), 3).transpose(0, 1, 3, 2)
    s[:, ::2] = few[:, ::2]
    s[:, 1::4, :, 1::2] = np.roll(s[:, 1::4, :, 0::2], 5, axis=2)
    s[:, 3] = W - 1 - rng.integers(0, 40, (N, 16, L))
    k[:, 1::2, 8:] = k[:, 1::2, :8]
    x = np.take_along_axis(rng.choice(np.array([0, 128, 255]), (N, 8, 16, 5)), rng.integers(0, 5, (N, 8, 1, W)), 3)
    return pack(r, x, k, s)
def setup_inputs_full(rng):
    r, x, k, s = parts(rng); own = np.arange(W); lane = np.arange(L); bag = (own >> 4) & 15
    z = 2 * rng.integers(0, 8, N) + 1
    r[:, :3] = rng.integers(0, 5, (N, 3, 16, W))
    even = own[(own & 16) == 0]; r[:, 1, bag[even], even] = 15; k[:, 1] = k[:, 1] | 16
    hot = np.repeat((bag[None, :] == z[:, None])[:, None, :], 8, axis=1)
    hot[:, :2, :256] = False; hot[:, 2, :256:2] = False
    r = np.where(hot[:, :, None, :], 15, r)
    named = np.take_along_axis(hot, k.reshape(N, 8, 16 * W), 2).reshape(N, 8, 16, W); k = np.where(named, k ^ 32, k)
    s[:, :3] = lane + 256 * rng.integers(0, W // 256, (N, 3, 16, L))
    inbag = (lane >> 4)[None, :] == z[:, None]
    first = np.arange(16)[:, None] == ((5 * (lane & 15)) & 15)[None, :]
    s = np.where(inbag[:, None, None, :], lane + 256 * np.where(first, 0, rng.integers(1, W // 256, (N, 8, 16, L))), s)
    return pack(r, x, k, s)
def check_inputs(d):
    bad = []
    for k, lo, hi in (("rec", 0, 15), ("wealth", 0, 255), ("kin", 0, W - 1), ("slips", 0, W - 1)):
        v = np.asarray(d[k]).astype(np.float64)
        if not (np.min(v) >= lo and np.max(v) <= hi): bad.append("range of " + k)
        elif np.any(v != np.floor(v)): bad.append("whole numbers of " + k)
    return bad
def reference(rec, wealth, kin, slips):
    R = rec.astype(np.float32).astype(np.int64).reshape(N, 8, 16, W); X = wealth.astype(np.float32).astype(np.int64).reshape(N, 8, 16, W)
    K = kin.astype(np.int64).reshape(N, 8, 16, W); S = slips.astype(np.int64).reshape(N, 8, 16, L)
    lane = np.arange(L); b = lane >> 4; j = lane & 15; a = np.zeros((N, 16), np.int64)
    lower = lane[None, :] < lane[:, None]
    def picks(tab, ks):
        return np.take_along_axis(tab, ks.reshape(8, 1, 16 * L), 2).reshape(8, 16, 16, L)
    for t in range(RO):
        T = 8 + t; later = []
        for r in range(N):
            o = (a[r][b] + 5 * j + t) & 15
            c = S[r][:, o, lane]
            ci = c[:, None, :]
            counts = ~np.any((c[:, :, None] == c[:, None, :]) & lower[None], axis=2)
            kc = np.take_along_axis(K[r], ci, 2)
            M = np.maximum(np.take_along_axis(R[r], ci, 2), np.max(picks(R[r], kc), axis=2))
            for u in range(P):
                q = (r + 1 + (P * t + u) % (N - 1)) % N
                M = np.maximum(M, np.max(picks(R[q], np.take_along_axis(K[q], ci, 2)), axis=2))
            f = np.sum(M >= T - 2, axis=1)
            bar = (M[:, b, lane] >= T - 3) | (f >= 8)
            barred = counts & bar; inst = counts & ~bar
            torn = inst | (barred & (f >= 12))
            nxt = np.zeros((8, L), bool); nxt[:, :L - 16] = torn[:, 16:]
            moved = barred & (f < 12) & ((f & 1) == 1) & nxt
            sc = np.sum(np.maximum(picks(X[r], kc) - np.take_along_axis(X[r], ci, 2)[:, :, None, :], 0), axis=1)
            best = np.take_along_axis(kc, np.argmax(sc, axis=1)[:, None, :], 1)[:, 0]
            new = np.where(torn | moved, best, c)
            new[:, 16:] = np.where(moved[:, :L - 16], c[:, :L - 16], new[:, 16:])
            later.append((o, c, inst, new))
        for r in range(N):
            o, c, inst, new = later[r]
            S[r][:, o, lane] = new
            gi, li = np.nonzero(inst)
            R[r][gi, b[li], c[gi, li]] = T
            K[r][gi, t, c[gi, li]] = c[gi, li ^ 1]
            a[r] = np.sum(inst.reshape(8, 16, 16), axis=(0, 2))
    return {"yr": R.reshape(N, 128, W).astype(np.float32).astype(BF), "ys": S.reshape(N, 128, L).astype(np.float32)}

@@ -1,0 +1,452 @@
+import numpy as np
+import math
+from concourse.mybir import dt, AluOpType, AxisListType, ActivationFunctionType
+
+W, NR = 1408, 5
+WD = W + 256
+NS = 6
+OWN_S = ((0, 64), (64, 128), (128, 192), (192, 224))
+OWN_V = (224, 256)
+ASK = ((0, 64), (64, 128), (128, 192), (192, 256))
+
+SCRATCH = {
+    "Kw": ("sbuf", [128, WD], "int32"), "Vw": ("sbuf", [128, WD], "bfloat16"), "Rw": ("sbuf", [128, WD], "bfloat16"),
+    "Xw": ("sbuf", [128, W], "bfloat16"), "recb": ("sbuf", [128, W], "bfloat16"),
+    "lnb": ("sbuf", [128, W], "float32"), "r24": ("sbuf", [128, W], "bfloat16"),
+    "T0": ("sbuf", [128, 256], "int32"), "T0h": ("sbuf", [128, 256], "float16"), "SLd": ("sbuf", [128, 512], "float16"),
+    "SL": ("sbuf", [128, 256], "float32"),
+    "ones": ("sbuf", [128, 256], "bfloat16"), "L16": ("sbuf", [128, 128], "bfloat16"), "R16b": ("sbuf", [128, 256], "bfloat16"),
+    "R16j": ("sbuf", [128, 256], "bfloat16"), "L8": ("sbuf", [128, 128], "bfloat16"), "Z8": ("sbuf", [128, 144], "bfloat16"),
+    "G88": ("sbuf", [128, 8], "bfloat16"), "Ib": ("sbuf", [128, 128], "bfloat16"), "I16": ("sbuf", [128, 128], "float16"),
+    "E": ("sbuf", [128, 256], "bfloat16"), "BOb": ("sbuf", [128, 128], "bfloat16"), "BO16": ("sbuf", [128, 128], "float16"),
+    "TRb": ("sbuf", [128, 128], "bfloat16"), "TR16": ("sbuf", [128, 128], "float16"), "Zw": ("sbuf", [128, 144], "bfloat16"),
+    "Gs": ("sbuf", [128, 8], "bfloat16"), "G16": ("sbuf", [128, 8], "float16"), "Cm": ("sbuf", [128, 256], "bfloat16"),
+    "NDH": ("sbuf", [128, 256], "float32"), "DT": ("sbuf", [128, 1024], "bfloat16"), "DTH": ("sbuf", [128, 1280], "float32"),
+    "D11": ("sbuf", [128, 256], "bfloat16"), "D12": ("sbuf", [128, 256], "bfloat16"),
+    "Dr": ("sbuf", [128, 2048], "float16"), "ND": ("sbuf", [128, 512], "float16"), "LT": ("sbuf", [128, 512], "float16"),
+    "nE": ("sbuf", [128, 16], "float32"), "negE": ("sbuf", [128, 16], "float32"),
+    "seg": ("sbuf", [128, 256], "bfloat16"), "RL1": ("sbuf", [128, 16], "uint16"), "RL2": ("sbuf", [128, 16], "uint16"),
+    "RL3": ("sbuf", [128, 16], "uint16"), "i1": ("sbuf", [128, 16], "int32"), "i2": ("sbuf", [128, 16], "int32"),
+    "i3": ("sbuf", [128, 16], "int32"), "pm": ("sbuf", [128, 16], "int32"), "pmf": ("sbuf", [128, 16], "float32"),
+    "dq": ("sbuf", [128, 16], "float32"), "dum": ("sbuf", [128, 16], "float32"), "basec": ("sbuf", [128, 1], "float32"),
+    "m16": ("sbuf", [128, 16], "bfloat16"), "mk4": ("sbuf", [128, 16], "float32"),
+    "offs": ("sbuf", [128, 16], "uint16"), "yo": ("sbuf", [128, 1], "int32"), "ya": ("sbuf", [128, 1], "int32"),
+    "ca": ("sbuf", [128, 17], "float32"), "cb": ("sbuf", [128, 17], "float32"), "c1": ("sbuf", [128, 16], "float32"),
+    "cE": ("sbuf", [128, 256], "float16"), "crow": ("sbuf", [128, 512], "float16"),
+    "kc": ("sbuf", [128, 256], "uint16"), "kcq": ("sbuf", [128, 256], "uint16"), "kc16": ("sbuf", [128, 256], "float16"),
+    "XC": ("sbuf", [128, 256], "bfloat16"), "XCr": ("sbuf", [128, 4096], "bfloat16"), "VC": ("sbuf", [128, 256], "bfloat16"),
+    "Vg": ("sbuf", [128, 4096], "bfloat16"), "Vq": ("sbuf", [128, 4096], "bfloat16"), "Dx": ("sbuf", [128, 4096], "bfloat16"),
+    "EQ": ("sbuf", [128, 2176], "bfloat16"), "UU": ("sbuf", [128, 768], "bfloat16"), "nK": ("sbuf", [128, 256], "float32"),
+    "nR": ("sbuf", [128, 256], "bfloat16"),
+    "y": ("sbuf", [128, 256], "float32"), "eqn": ("sbuf", [128, 256], "bfloat16"), "neq": ("sbuf", [128, 256], "bfloat16"),
+    "ek": ("sbuf", [128, 256], "float32"), "s2": ("sbuf", [128, 256], "float32"), "Bx": ("sbuf", [128, 256], "float16"),
+    "Bf": ("sbuf", [128, 48], "float32"), "sm": ("sbuf", [128, 256], "float32"), "gq": ("sbuf", [128, 16], "float32"),
+    "wi": ("sbuf", [128, 16], "int32"), "pp": ("sbuf", [128, 16], "int32"), "nirep": ("sbuf", [128, 128], "bfloat16"),
+    "NT": ("sbuf", [128, 17], "float32"), "mv": ("sbuf", [128, 17], "float32"), "nw": ("sbuf", [128, 16], "float32"),
+    "msk": ("sbuf", [128, 256], "float16"), "ltm": ("sbuf", [128, 256], "float16"), "SLz": ("sbuf", [128, 256], "float16"),
+    "nm": ("sbuf", [128, 256], "float16"), "ysb": ("sbuf", [128, 256], "float32"),
+}
+for _t in range(NR):
+    SCRATCH["cu%d" % _t] = ("sbuf", [128, 16], "uint16")
+    SCRATCH["rcv%d" % _t] = ("sbuf", [128, 16], "uint16")
+    SCRATCH["rep%d" % _t] = ("sbuf", [128, 256], "bfloat16")
+    SCRATCH["rrv%d" % _t] = ("sbuf", [128, 256], "bfloat16")
+    SCRATCH["scl%d" % _t] = ("sbuf", [128, 16], "uint16")
+for _k in range(8):
+    SCRATCH["P%d" % _k] = ("psum", [128, 512], "float32")
+SEMAPHORES = ["v", "s", "t", "g", "dsl", "dk", "dr", "dx", "loc", "dout"] + ["rl%d" % t for t in range(NR)] + ["rr%d" % t for t in range(NR)]
+
+
+def rank_program(g, core, T, topo):
+    rank = T.rank_of(core)
+    if rank is None:
+        return
+    A, F = AluOpType, ActivationFunctionType
+    queues = {"v": g.vector, "s": g.scalar, "t": g.tensor, "g": g, "y": g.sync}
+    cnt = {}
+    seen = {q: {} for q in queues}
+    snap = {}
+    lastw, readers, bank = {}, {}, {}
+
+    def wait(q, tok):
+        sem, val = tok
+        if seen[q].get(sem, 0) >= val:
+            return
+        queues[q].wait_ge(T.sem[sem], val)
+        seen[q][sem] = val
+        for s, x in snap.get(tok, {}).items():
+            if seen[q].get(s, 0) < x:
+                seen[q][s] = x
+
+    def deps(q, r, w, bk):
+        need = {}
+
+        def add(tok):
+            if tok is not None and need.get(tok[0], 0) < tok[1]:
+                need[tok[0]] = tok[1]
+        for k in r:
+            tok = lastw.get(k)
+            if tok is not None and not (q == "t" and tok[0] == "t"):
+                add(tok)
+        for k in w:
+            tok = lastw.get(k)
+            if tok is not None and not (q == "t" and tok[0] == "t"):
+                add(tok)
+            for x, tok in readers.get(k, {}).items():
+                if x != q:
+                    add(tok)
+        for b in bk:
+            for x, tok in bank.get(b, {}).items():
+                if x != q:
+                    add(tok)
+        for s in sorted(need):
+            wait(q, (s, need[s]))
+
+    def note(q, tok, r, w, bk):
+        snap[tok] = dict(seen[q])
+        for k in r:
+            readers.setdefault(k, {})[q] = tok
+        for k in w:
+            lastw[k] = tok
+            readers[k] = {}
+        for b in bk:
+            bank.setdefault(b, {})[q] = tok
+
+    def op(q, fn, r=(), w=(), bk=()):
+        deps(q, r, w, bk)
+        fn(queues[q]).then_inc(T.sem[q], 1)
+        cnt[q] = cnt.get(q, 0) + 1
+        note(q, (q, cnt[q]), r, w, bk)
+
+    def dma(q, sem, out, in_, r=(), w=()):
+        deps(q, r, w, ())
+        queues[q].dma_start(out, in_).then_inc(T.sem[sem], 16)
+        cnt[sem] = cnt.get(sem, 0) + 16
+        for k in w:
+            lastw[k] = (sem, cnt[sem])
+
+    def mm(out, lhsT, rhs, start, stop, r=(), w=(), bk=()):
+        op("t", lambda e: e.matmul(out, lhsT, rhs, start, stop), r, w, bk)
+
+    def cp(q, out, in_, r, w, bk=()):
+        if q == "s":
+            op("s", lambda e: e.activation(out, in_, F.Copy), r, w, bk)
+        else:
+            op("v", lambda e: e.tensor_copy(out, in_), r, w, bk)
+
+    def tt(out, a, b, o, r, w, bk=()):
+        op("v", lambda e: e.tensor_tensor(out, a, b, o), r, w, bk)
+
+    def ts(out, a, s1, s2, o0, o1, r, w, bk=()):
+        if o1 is None:
+            op("v", lambda e: e.tensor_scalar(out, a, s1, None, o0), r, w, bk)
+        else:
+            op("v", lambda e: e.tensor_scalar(out, a, s1, s2, o0, o1), r, w, bk)
+
+    def act(out, in_, f, r, w, bk=(), bias=0.0, scale=1.0):
+        op("s", lambda e: e.activation(out, in_, f, bias=bias, scale=scale), r, w, bk)
+
+    def fill(ap, val, w):
+        op("v", lambda e: e.memset(ap, val), (), w)
+
+    def sel(out, in_, pat, o, base, cm, r, w):
+        op("g", lambda e: e.affine_select(out, in_, pat, o, 0.0, base, cm), r, w)
+
+    def send(out, in_, rsem, dst, r):
+        deps("g", r, (), ())
+        eng = topo.engines(core, dst)[:8]
+        rid, pid = topo.addr(dst, core)
+        g.remote_dma(out, in_, T.sem[rsem], T.sem.loc, pid, rid, sum(1 << e for e in eng))
+        cnt["loc"] = cnt.get("loc", 0) + len(eng)
+
+    for k in range(16):
+        gg, h = k // 2, k % 2
+        dma("y" if h == 0 else "s", "dsl", T.T0[:, 128 * h + 16 * gg:128 * h + 16 * gg + 16],
+            T.slips[16 * gg + 8 * h:16 * gg + 8 * h + 8, :], w=("T0",))
+    dma("y", "dk", T.Kw[:, 0:W], T.kin[:, :], w=("Kw",))
+    dma("s", "dr", T.recb[:], T.rec[:, :], w=("recb",))
+    dma("s", "dx", T.Xw[:], T.wealth[:, :], w=("Xw",))
+
+    fill(T.ones[:], 1.0, ("ones",))
+    sel(T.Ib[:], T.ones[:, 0:128], [[-1, 128]], A.is_equal, 0, 1, ("ones",), ("Ib",))
+    sel(T.L16[0:16, :], T.ones[0:16, 0:128], [[0, 8], [1, 16]], A.is_equal, 0, -1, ("ones",), ("L16",))
+    sel(T.R16j[0:16, :], T.ones[0:16, :], [[0, 16], [1, 16]], A.is_equal, 0, -1, ("ones",), ("R16j",))
+    op("g", lambda e: e.iota(T.i1[:], [[0, 16]], 0, 1), (), ("i1",))
+    sel(T.L8[0:8, :], T.ones[0:8, 0:128], [[1, 8], [0, 16]], A.is_equal, 0, -1, ("ones",), ("L8",))
+    op("g", lambda e: e.iota(T.i2[:], [[1, 16]], 0, 0), (), ("i2",))
+    sel(T.R16b[0:16, :], T.ones[0:16, :], [[1, 16], [0, 16]], A.is_equal, 0, -1, ("ones",), ("R16b",))
+    sel(T.Z8[0:8, :], T.ones[0:8, 0:144], [[1, 144]], A.is_equal, -15, -16, ("ones",), ("Z8",))
+    sel(T.G88[0:8, :], T.ones[0:8, 0:8], [[1, 8]], A.is_equal, 0, -1, ("ones",), ("G88",))
+    op("g", lambda e: e.iota(T.i3[:], [[16, 16]], 15, 0), (), ("i3",))
+    op("g", lambda e: e.iota(T.dq[:], [[16, 16]], W, 0, allow_small_or_imprecise_dtypes=True), (), ("dq",))
+    op("g", lambda e: e.iota(T.Cm[:], [[0, 16], [-1, 16]], 15, 0, allow_small_or_imprecise_dtypes=True), (), ("Cm",))
+
+    fill(T.seg[:], 1.0, ("seg",))
+    fill(T.seg[:, 0:256:16], 0.0, ("seg",))
+    fill(T.m16[:], -16.0, ("m16",))
+    fill(T.mk4[:], 4096.0, ("mk4",))
+    fill(T.NT[:], 1.0, ("NT",))
+    fill(T.mv[:], 0.0, ("mv",))
+    fill(T.ca[:], 0.0, ("ca",))
+    fill(T.cb[:], 0.0, ("cb",))
+    ts(T.LT[:, 0:256], T.ones[:], 0.0, None, A.mult, None, ("ones",), ("LT",))
+    ts(T.LT[:, 256:512], T.ones[:], 0.0, None, A.mult, None, ("ones",), ("LT",))
+
+    cp("v", T.I16[:], T.Ib[:], ("Ib",), ("I16",))
+    mm(T.P0[:, 0:256], T.L16[0:16, :], T.R16j[0:16, :], True, True, ("L16", "R16j"), ("pE",), ("P0",))
+    cp("v", T.E[:], T.P0[:, 0:256], ("pE",), ("E",), ("P0",))
+    for j in range(16):
+        r = 5 * j % 16
+        ts(T.Dr[:, 128 * r:128 * r + 128], T.I16[:], T.E[:, j:j + 1], None, A.mult, None, ("I16", "E"), ("Dr",))
+    cp("v", T.T0h[:], T.T0[:], ("T0",), ("T0h",))
+    for h in range(2):
+        mm(T.P2[:, 128 * h:128 * h + 128], T.T0h[:, 128 * h:128 * h + 128], T.I16[:], True, True, ("T0h", "I16"), ("pT0",), ("P2",))
+    for h in range(2):
+        cp("v", T.SLd[:, 256 * h:256 * h + 256], T.P2[:, 0:256], ("pT0",), ("SLd",), ("P2",))
+    for r in range(16):
+        mm(T.P3[:, 0:16], T.Dr[:, 128 * r:128 * r + 128], T.SLd[:, 16 * r:16 * r + 16], r == 0, r == 15, ("Dr", "SLd"), ("pc0",), ("P3",))
+    cp("v", T.cu0[:], T.P3[:, 0:16], ("pc0",), ("cu0",), ("P3",))
+    send(T.rcv0[:], T.cu0[:], "rl0", T.cores[(rank + 1) % 6], ("cu0",))
+    cp("v", T.ca[:, 1:17], T.P3[:, 0:16], ("pc0",), ("ca",), ("P3",))
+    act(T.Vw[:, 0:W], T.recb[:], F.Exp, ("recb",), ("Vw",), bias=0.0, scale=6.0 * math.log(2.0))
+    mm(T.P1[:, 0:128], T.L8[0:8, :], T.L8[0:8, :], True, True, ("L8",), ("pB",), ("P1",))
+    mm(T.P1[:, 128:272], T.L8[0:8, :], T.Z8[0:8, :], True, True, ("L8", "Z8"), ("pB",), ("P1",))
+    mm(T.P1[:, 272:280], T.L8[0:8, :], T.G88[0:8, :], True, True, ("L8", "G88"), ("pB",), ("P1",))
+    mm(T.P0[:, 256:512], T.L16[0:16, :], T.R16b[0:16, :], True, True, ("L16", "R16b"), ("pD",), ("P0",))
+
+    def setup_vector():
+        ts(T.pm[:], T.i1[:], 15, None, A.bitwise_and, None, ("i1",), ("pm",))
+        cp("v", T.RL1[:], T.i2[:], ("i2",), ("RL1",))
+        cp("v", T.BO16[:], T.P1[:, 0:128], ("pB",), ("BO16",), ("P1",))
+        cp("v", T.BOb[:], T.P1[:, 0:128], ("pB",), ("BOb",), ("P1",))
+        sel(T.TRb[:], T.BOb[:], [[-1, 128]], A.is_gt, 0, 1, ("BOb",), ("TRb",))
+        cp("v", T.RL3[:], T.pm[:], ("pm",), ("RL3",))
+        cp("v", T.pmf[:], T.pm[:], ("pm",), ("pmf",))
+        cp("v", T.RL2[:], T.i3[:], ("i3",), ("RL2",))
+        ts(T.Gs[:], T.P1[:, 272:280], 16.0, None, A.mult, None, ("pB",), ("Gs",), ("P1",))
+        cp("v", T.G16[:], T.P1[:, 272:280], ("pB",), ("G16",), ("P1",))
+        cp("v", T.Zw[:], T.P1[:, 128:272], ("pB",), ("Zw",), ("P1",))
+        ts(T.NDH[:], T.P0[:, 256:512], -1e29, 1e29, A.mult, A.add, ("pD",), ("NDH",), ("P0",))
+        ts(T.dum[:], T.dq[:], T.pmf[:, 0:1], None, A.add, None, ("dq", "pmf"), ("dum",))
+        ts(T.basec[:], T.pmf[:, 0:1], 2048.0, None, A.add, None, ("pmf",), ("basec",))
+        ts(T.nE[:], T.E[:, 0:16], -1.0, 1.0, A.mult, A.add, ("E",), ("nE",))
+        ts(T.negE[:], T.E[:, 0:16], -1.0, None, A.mult, None, ("E",), ("negE",))
+        cp("v", T.offs[:, 0:1], T.pm[:, 0:1], ("pm",), ("off0",))
+        for t in range(4):
+            cp("v", T.LT[:, 128 * t + t:128 * t + 128:16], T.BO16[:, t:128:16], ("BO16", "LT"), ("LTx",))
+            ts(T.ND[:, 128 * t:128 * t + 128], T.I16[:], T.nE[:, t:t + 1], None, A.mult, None, ("I16", "nE"), ("ND",))
+        cp("v", T.TR16[:], T.TRb[:], ("TRb",), ("TR16",))
+
+    def setup_scalar():
+        for t in range(4):
+            act(T.DT[:, 256 * t:256 * t + 256], T.P0[:, 256:512], F.Copy, ("pD",), ("DT",), ("P0",), scale=2.0 ** (6 * (8 + t)))
+        for t, n in ((11, "D11"), (12, "D12")):
+            act(T[n][:], T.P0[:, 256:512], F.Copy, ("pD",), (n,), ("P0",), scale=float(t))
+
+    for t in range(NR):
+        last = t == NR - 1
+        cn = "ca" if t % 2 == 0 else "cb"
+        C = T[cn]
+        c, cprev = C[:, 1:17], C[:, 0:16]
+        cu, rcv, scl = T["cu%d" % t], T["rcv%d" % t], T["scl%d" % t]
+        cuk, rcvk, sclk = "cu%d" % t, "rcv%d" % t, "scl%d" % t
+        q = T.cores[(rank + 1 + t % 5) % 6]
+        p = T.cores[(rank - 1 - t % 5) % 6]
+        lastw[rcvk] = ("rl%d" % t, 8)
+        lastw["rrv%d" % t] = ("rr%d" % t, 8)
+
+        cp("v", T.kc[:], T.Kw[:, 0:W].indirect(cu[:]), ("Kw", cuk), ("kc",))
+        if t > 0:
+            ts_ = t - 1
+            pcl = T["scl%d" % ts_]
+            tt(T.Vw[:].indirect(pcl[:]), T.VC[:], T.DT[:, 256 * ts_:256 * ts_ + 256], A.add, ("VC", "DT", "scl%d" % ts_), ("Vw",))
+        else:
+            setup_vector()
+        cp("s", T.XC[:], T.Xw[:].indirect(cu[:]), ("Xw", cuk), ("XC",))
+        for m in range(NS):
+            cp("s", T.XCr[:, m:4096:16], T.XC[:], ("XC",), ("XCr%d" % m,))
+        cp("s", T.VC[:], T.Vw[:, 0:W].indirect(cu[:]), ("Vw", cuk), ("VC",))
+        cp("v", T.kcq[:], T.Kw[:, 0:W].indirect(rcv[:]), ("Kw", rcvk), ("kcq",))
+        ts(T.c1[:], c, 1.0, None, A.add, None, (cn,), ("c1",))
+        cp("v", T.kc16[:], T.kc[:], ("kc",), ("kc16",))
+        tt(T.cE[:], T.c1[:].indirect(T.RL1[:]), T.E[:], A.mult, ("c1", "RL1", "E"), ("cE",))
+        mm(T.P4[:, 0:256], T.BO16[:], T.cE[:], True, True, ("BO16", "cE"), ("pcrow",), ("P4",))
+        mm(T.P4[:, 256:512], T.TR16[:], T.cE[:], True, True, ("TR16", "cE"), ("pcrow",), ("P4",))
+        for h in range(2):
+            mm(T.P3[:, 128 * h:128 * h + 128], T.kc16[:, 128 * h:128 * h + 128], T.I16[:], True, True, ("kc16", "I16"), ("pkc",), ("P3",))
+        if not last:
+            mm(T.P3[:, 256:512], T.ND[:, 128 * t:128 * t + 128], T.kc16[:], True, False, ("ND", "kc16"), ("pnK",), ("P3",))
+            mm(T.P3[:, 256:512:2], T.LT[:, 128 * t:128 * t + 128], T.cE[:, 1:256:2], False, False, ("LTx", "cE"), ("pnK",), ("P3",))
+            mm(T.P3[:, 257:512:2], T.LT[:, 128 * t:128 * t + 128], T.cE[:, 0:256:2], False, True, ("LTx", "cE"), ("pnK",), ("P3",))
+        for m in range(NS, 16):
+            cp("v", T.XCr[:, m:4096:16], T.XC[:], ("XC",), ("XCr%d" % m,))
+        cp("v", T.crow[:], T.P4[:], ("pcrow",), ("crow",), ("P4",))
+        if last:
+            cp("v", T.SL[:].indirect(T.offs[:, 2 * t:2 * t + 1]), T.mk4[:], ("mk4", "off%d" % t, cn, cuk), ("SL",))
+            for h in range(2):
+                cp("v", T.SLd[:, 256 * h:256 * h + 256], T.SL[:], ("SL",), ("SLd",))
+            ts(T.Rw[:, 0:W], T.r24[:], 16.0, None, A.subtract, None, ("r24",), ("Rw",))
+
+        mm(T.P0[:, 0:256], T.Ib[:], T.VC[:], True, False, ("Ib", "VC"), ("pS",), ("P0",))
+        for k, (a, b) in enumerate(ASK):
+            cp("s", T.Vq[:, 16 * a:16 * b], T.Vw[:, 0:W].indirect(T.kcq[:, a:b]), ("Vw", "kcq"), ("Vq%d" % k,))
+            for m in range(16):
+                mm(T.P1[:, a:b], T.Ib[:], T.Vq[:, 16 * a + m:16 * b:16], m == 0, m == 15, ("Ib", "Vq%d" % k), ("pA",), ("P1",))
+        if t == 0:
+            for r in range(16):
+                mm(T.P5[:, 0:256], T.Dr[:, 128 * r:128 * r + 128], T.SLd[:, 16 * r:16 * r + 256], r == 0, r == 15, ("Dr", "SLd"), ("pSL",), ("P5",))
+
+        def own_mm(k, a, b):
+            for m in range(16):
+                mm(T.P0[:, a:b], T.Ib[:], T.Vg[:, 16 * a + m:16 * b:16], False, False, ("Ib", "Vg%d" % k), ("pS",), ("P0",))
+
+        def own_s(k):
+            a, b = OWN_S[k]
+            cp("s", T.Vg[:, 16 * a:16 * b], T.Vw[:, 0:W].indirect(T.kc[:, a:b]), ("Vw", "kc"), ("Vg%d" % k,))
+
+        def wealth_half(h):
+            tt(T.Dx[:, 2048 * h:2048 * h + 2048], T.Xw[:].indirect(T.kc[:, 128 * h:128 * h + 128]), T.XCr[:, 2048 * h:2048 * h + 2048],
+               A.max, ("Xw", "kc") + tuple("XCr%d" % m for m in range(16)), ("Dx%d" % h,))
+
+        def score_mm(h):
+            mm(T.P2[:, 128 * h:128 * h + 128], T.Ib[:], T.Cm[:, 128 * h:128 * h + 128], True, False, ("Ib", "Cm"), ("pKey",), ("P2",))
+            for m in range(16):
+                mm(T.P2[:, 128 * h + m:128 * h + 128:16], T.Dx[:, 2048 * h + m:2048 * h + 2048:16], T.Gs[:], False, m == 15,
+                   ("Dx%d" % h, "Gs"), ("pKey",), ("P2",))
+
+        eqo = [256]
+        eqpos = []
+        for b in range(15):
+            eqpos.append(eqo[0])
+            eqo[0] += 16 * (15 - b)
+
+        def eq_v(lo, hi):
+            for b in range(lo, hi):
+                n = 16 * (15 - b)
+                ts(T.EQ[:, eqpos[b]:eqpos[b] + n], T.crow[:, 16 * b + 16:256], T.c1[:, b:b + 1], None, A.is_equal, None, ("crow", "c1"), ("EQ%d" % b,))
+
+        def eq_mm(lo, hi):
+            for b in range(lo, hi):
+                n = 16 * (15 - b)
+                mm(T.P5[:, 16 * b + 16:256], T.BOb[:], T.EQ[:, eqpos[b]:eqpos[b] + n], False, b == 14, ("BOb", "EQ%d" % b), ("pcnt",), ("P5",))
+
+        own_s(0)
+        cp("s", T["rep%d" % t][:], T.P1[:, 0:256], ("pA",), ("rep%d" % t,), ("P1",))
+        send(T["rrv%d" % t][:], T["rep%d" % t][:], "rr%d" % t, p, ("rep%d" % t,))
+        own_s(1)
+        if t == 0:
+            setup_scalar()
+        act(T.DTH[:, 256 * t:256 * t + 256], T.NDH[:], F.Copy, ("NDH",), ("DTH%d" % t,), bias=2.0 ** (6 * (8 + t - 3)))
+        if not last:
+            act(T.nK[:], T.P3[:, 256:512], F.Identity, ("pnK", "negE"), ("nK",), ("P3",), bias=T.negE[:, t:t + 1])
+        own_s(2)
+        own_s(3)
+
+        wealth_half(0)
+        score_mm(0)
+        own_mm(0, *OWN_S[0])
+        tt(T.EQ[:, 0:256], T.c1[:].indirect(T.RL1[:]), T.crow[:, 256:512], A.is_equal, ("c1", "RL1", "crow"), ("EQin",))
+        if t == 0:
+            cp("v", T.SL[:], T.P5[:, 0:256], ("pSL",), ("SL",), ("P5",))
+        eq_v(0, 8)
+        mm(T.P5[:, 0:256], T.BOb[:], T.EQ[:, 0:256], True, False, ("BOb", "EQin"), ("pcnt",), ("P5",))
+        eq_mm(0, 8)
+        own_mm(1, *OWN_S[1])
+        wealth_half(1)
+        if last:
+            for r in range(16):
+                x = 16 * ((16 - r) % 16)
+                mm(T.P7[:, 0:256], T.Dr[:, 128 * r:128 * r + 128], T.SLd[:, x:x + 256], r == 0, r == 15, ("Dr", "SLd"), ("pSU",), ("P7",))
+        own_mm(2, *OWN_S[2])
+        score_mm(1)
+        eq_v(8, 15)
+        eq_mm(8, 15)
+        act(T.UU[:, 512:768], T.P5[:, 0:256], F.Copy, ("pcnt",), ("UUn",), ("P5",), scale=4.0)
+        a, b = OWN_V
+        cp("v", T.Vg[:, 16 * a:16 * b], T.Vw[:, 0:W].indirect(T.kc[:, a:b]), ("Vw", "kc"), ("Vg4",))
+        own_mm(3, *OWN_S[3])
+        own_mm(4, a, b)
+        if t == 3:
+            act(T.lnb[:], T.Vw[:, 0:W], F.Ln, ("Vw",), ("lnb",), scale=2.0 ** -48)
+            act(T.r24[:], T.lnb[:], F.Copy, ("lnb",), ("r24",), scale=1.0 / (6.0 * math.log(2.0)), bias=24.0)
+        if last:
+            tt(T.nR[:], T.Rw[:, 0:W].indirect(T.cu3[:]), T.D11[:], A.max, ("Rw", "cu3", "D11"), ("nR",))
+            cp("v", T.Rw[:].indirect(T.scl3[:]), T.nR[:], ("nR", "scl3", "Rw"), ("Rw",))
+            tt(T.nR[:], T.Rw[:, 0:W].indirect(cu[:]), T.D12[:], A.max, ("Rw", cuk, "D12"), ("nR",))
+            ts(T.msk[:], T.P7[:, 0:256], 4096.0, None, A.is_ge, None, ("pSU",), ("msk",), ("P7",))
+            ts(T.ltm[:], T.P7[:, 0:256], 4096.0, None, A.is_lt, None, ("pSU",), ("ltm",), ("P7",))
+        op("v", lambda e: e.tensor_tensor_scan(T.y[:], T.seg[:], T.P2[:, 0:256], 0.0, A.mult, A.max), ("seg", "pKey"), ("y",), ("P2",))
+        if last:
+            tt(T.SLz[:], T.P7[:, 0:256], T.ltm[:], A.mult, ("pSU", "ltm"), ("SLz",), ("P7",))
+        tt(T.eqn[:], T.P2[:, 0:256], T.y[:], A.is_equal, ("pKey", "y"), ("eqn",), ("P2",))
+        tt(T.neq[:], T.P2[:, 0:256], T.y[:], A.not_equal, ("pKey", "y"), ("neq",), ("P2",))
+        tt(T.ek[:], T.P3[:, 0:256], T.eqn[:], A.mult, ("pkc", "eqn"), ("ek",), ("P3",))
+        op("v", lambda e: e.tensor_tensor_scan(T.s2[:], T.neq[:], T.ek[:], 0.0, A.mult, A.add), ("neq", "ek"), ("s2",))
+        tt(T.Bx[:], T.s2[:].indirect(T.RL2[:]), T.E[:], A.mult, ("s2", "RL2", "E"), ("Bx",))
+        for h in range(2):
+            mm(T.P7[:, 256 + 8 * h:264 + 8 * h], T.Bx[:, 128 * h:128 * h + 128], T.G16[:], True, True, ("Bx", "G16"), ("pBest",), ("P7",))
+        mm(T.P0[:, 0:256], T.Ib[:], T["rrv%d" % t][:], False, True, ("Ib", "rrv%d" % t), ("pS",), ("P0",))
+        ts(T.UU[:, 0:256], T.P0[:, 0:256], 2.0 ** (6 * (8 + t - 2)), None, A.is_ge, None, ("pS",), ("UU2",), ("P0",))
+        tt(T.UU[:, 256:512], T.P0[:, 0:256], T.DTH[:, 256 * t:256 * t + 256], A.is_ge, ("pS", "DTH%d" % t), ("UU3",), ("P0",))
+        for j in range(16):
+            mm(T.P6[:, 0:48], T.Zw[:, 15 - j:143 - j], T.UU[:, j:768:16], j == 0, j == 15, ("Zw", "UU2", "UU3", "UUn"), ("pF",), ("P6",))
+        cp("v", T.Bf[:], T.P6[:, 0:48], ("pF",), ("Bf",), ("P6",))
+        sm = [T.sm[:, 16 * k:16 * k + 16] for k in range(16)]
+        tt(T.wi[:], T.Bf[:, 0:16], T.Bf[:, 32:48], A.add, ("Bf",), ("wi",))
+        ts(sm[0], T.Bf[:, 16:32], 8.0, None, A.mult, None, ("Bf",), ("d8",))
+        tt(T.gq[:], T.wi[:], sm[0], A.max, ("wi", "d8"), ("gq",))
+        ts(T.pp[:], T.wi[:], 1, None, A.bitwise_and, None, ("wi",), ("pp",))
+        ts(sm[1], T.wi[:], 12.0, None, A.is_lt, None, ("wi",), ("lt12",))
+        if not last:
+            ts(T.nirep[:], T.gq[:].indirect(T.RL3[:, 0:8]), 8.0, None, A.is_ge, None, ("gq", "RL3"), ("nirep",))
+            mm(T.P6[:, 64:65], T.nirep[:], T.m16[:, 0:1], True, True, ("nirep", "m16"), ("pOff",), ("P6",))
+        ts(sm[2], T.gq[:], 8.0, None, A.is_ge, None, ("gq",), ("ni",))
+        ts(sm[3], T.wi[:], 64.0, None, A.is_lt, None, ("wi",), ("lt64",))
+        tt(sm[4], T.pp[:], sm[1], A.mult, ("pp", "lt12"), ("m1",))
+        tt(sm[6], sm[2], T.dum[:], A.mult, ("ni", "dum"), ("nd",))
+        tt(sm[7], sm[3], sm[1], A.subtract, ("lt64", "lt12"), ("tb",))
+        tt(sm[5], sm[4], sm[2], A.mult, ("m1", "ni"), ("m2",))
+        tt(sm[8], sm[6], c, A.max, ("nd", cn), ("lst",))
+        tt(T.NT[:, 0:16], sm[2], sm[7], A.subtract, ("ni", "tb", "NT"), ("NT",))
+        cp("v", scl[:], sm[8], ("lst",), (sclk,))
+        tt(T.mv[:, 1:17], sm[5], T.NT[:, 1:17], A.is_gt, ("m2", "NT", "mv"), ("mv",))
+        if last:
+            cp("v", T.Rw[:].indirect(scl[:]), T.nR[:], ("nR", sclk, "Rw"), ("Rw",))
+            dma("y", "dout", T.yr[:, :], T.Rw[:, 0:W], r=("Rw",))
+        else:
+            ts(T.yo[:], T.P6[:, 64:65], T.basec[:, 0:1], float(16 * (t + 1)), A.add, A.add, ("pOff", "basec"), ("yo",), ("P6",))
+        tt(sm[9], T.NT[:, 0:16], T.mv[:, 1:17], A.is_gt, ("NT", "mv"), ("NM",))
+        tt(sm[11], T.mv[:, 0:16], cprev, A.mult, ("mv", cn), ("R2",))
+        if not last:
+            ts(T.ya[:], T.yo[:], 255, None, A.bitwise_and, None, ("yo",), ("ya",))
+        tt(sm[10], sm[9], c, A.mult, ("NM", cn), ("R1",))
+        tt(sm[12], sm[9], T.mv[:, 0:16], A.add, ("NM", "mv"), ("q1",))
+        tt(sm[13], sm[10], sm[11], A.add, ("R1", "R2"), ("R12",))
+        ts(sm[14], sm[12], -1.0, 1.0, A.mult, A.add, ("q1",), ("Bm",))
+        if not last:
+            cp("v", T.offs[:, 2 * t + 2:2 * t + 3], T.ya[:], ("ya",), ("off%d" % (t + 1),))
+        tt(sm[15], T.P7[:, 256:272], sm[14], A.mult, ("pBest", "Bm"), ("xb",), ("P7",))
+        tt(T.nw[:], sm[15], sm[13], A.add, ("xb", "R12"), ("nw",))
+        if not last:
+            cp("v", T.SL[:].indirect(T.offs[:, 2 * t:2 * t + 1]), T.nw[:], ("nw", "off%d" % t, "SL"), ("SL",))
+            n = t + 1
+            nn = "cb" if t % 2 == 0 else "ca"
+            cp("v", T["cu%d" % n][:], T.SL[:].indirect(T.offs[:, 2 * n:2 * n + 1]), ("SL", "off%d" % n), ("cu%d" % n,))
+            send(T["rcv%d" % n][:], T["cu%d" % n][:], "rl%d" % n, T.cores[(rank + 1 + n % 5) % 6], ("cu%d" % n,))
+            cp("v", T[nn][:, 1:17], T.SL[:].indirect(T.offs[:, 2 * n:2 * n + 1]), ("SL", "off%d" % n, nn), (nn,))
+            cp("v", T.Kw[:].indirect(scl[:]), T.nK[:], ("nK", sclk, "Kw"), ("Kw",))
+        else:
+            tt(T.nm[:], T.nw[:].indirect(T.RL3[:]), T.msk[:], A.mult, ("nw", "RL3", "msk"), ("nm",))
+            for h in range(2):
+                mm(T.P4[:, 128 * h:128 * h + 128], T.SLz[:, 128 * h:128 * h + 128], T.I16[:], True, False, ("SLz", "I16"), ("pY",), ("P4",))
+                mm(T.P4[:, 128 * h:128 * h + 128], T.nm[:, 128 * h:128 * h + 128], T.I16[:], False, True, ("nm", "I16"), ("pY",), ("P4",))
+            cp("v", T.ysb[:], T.P4[:, 0:256], ("pY",), ("ysb",), ("P4",))
+            for k in range(16):
+                gg, h = k // 2, k % 2
+                dma("y" if h == 0 else "s", "dout", T.ys[16 * gg + 8 * h:16 * gg + 8 * h + 8, :],
+                    T.ysb[:, 128 * h + 16 * gg:128 * h + 16 * gg + 16], r=("ysb",))
+    for s in ("v", "s", "t", "g", "dsl", "dk", "dr", "dx", "loc", "dout"):
+        wait("g", (s, cnt[s]))
+    for t in range(NR):
+        wait("g", ("rl%d" % t, 8))
+        wait("g", ("rr%d" % t, 8))

@@ -162,7 +162,7 @@ def rank_program(g, core, T, topo):
     for k in range(16):
         gg, h = k // 2, k % 2
         dma("y" if h == 0 else "s", "dsl", T.T0[:, 128 * h + 16 * gg:128 * h + 16 * gg + 16],
-            T.slips[16 * gg + 8 * h:16 * gg + 8 * h + 8, :], w=("T0",))
+            T.slips[16 * gg + 8 * h:16 * gg + 8 * h + 8, :], w=("T0_%d" % k,))
     dma("y", "dk", T.Kw[:, 0:W], T.kin[:, :], w=("Kw",))
     dma("s", "dr", T.recb[:], T.rec[:, :], w=("recb",))
     dma("s", "dx", T.Xw[:], T.wealth[:, :], w=("Xw",))
@@ -198,7 +198,7 @@ def rank_program(g, core, T, topo):
     for j in range(16):
         r = 5 * j % 16
         ts(T.Dr[:, 128 * r:128 * r + 128], T.I16[:], T.E[:, j:j + 1], None, A.mult, None, ("I16", "E"), ("Dr",))
-    cp("v", T.T0h[:], T.T0[:], ("T0",), ("T0h",))
+    cp("v", T.T0h[:], T.T0[:], tuple("T0_%d" % k for k in range(16)), ("T0h",))
     for h in range(2):
         mm(T.P2[:, 128 * h:128 * h + 128], T.T0h[:, 128 * h:128 * h + 128], T.I16[:], True, True, ("T0h", "I16"), ("pT0",), ("P2",))
     for h in range(2):

@@ -4,10 +4,11 @@ from concourse.mybir import dt, AluOpType, AxisListType, ActivationFunctionType
 
 W, NR = 1408, 5
 WD = W + 256
-NS = 6
-OWN_S = ((0, 64), (64, 128), (128, 192), (192, 224))
-OWN_V = (224, 256)
-ASK = ((0, 64), (64, 128), (128, 192), (192, 256))
+NS = 10
+OWN = ((0, 32), (32, 64), (64, 128), (128, 192), (192, 256))
+PRE, MID = 1, 2
+ASK = ((0, 96), (96, 160), (160, 192), (192, 256))
+ASKV, ASKO = (3,), (3, 0, 1, 2)
 
 SCRATCH = {
     "Kw": ("sbuf", [128, WD], "int32"), "Vw": ("sbuf", [128, WD], "bfloat16"), "Rw": ("sbuf", [128, WD], "bfloat16"),
@@ -21,16 +22,17 @@ SCRATCH = {
     "E": ("sbuf", [128, 256], "bfloat16"), "BOb": ("sbuf", [128, 128], "bfloat16"), "BO16": ("sbuf", [128, 128], "float16"),
     "TRb": ("sbuf", [128, 128], "bfloat16"), "TR16": ("sbuf", [128, 128], "float16"), "Zw": ("sbuf", [128, 144], "bfloat16"),
     "Gs": ("sbuf", [128, 8], "bfloat16"), "G16": ("sbuf", [128, 8], "float16"), "Cm": ("sbuf", [128, 256], "bfloat16"),
-    "NDH": ("sbuf", [128, 256], "float32"), "DT": ("sbuf", [128, 1024], "bfloat16"), "DTH": ("sbuf", [128, 1280], "float32"),
+    "Dm": ("sbuf", [128, 256], "bfloat16"), "NDH": ("sbuf", [128, 256], "float32"), "DT": ("sbuf", [128, 1024], "bfloat16"), "DTH": ("sbuf", [128, 1280], "float32"),
     "D11": ("sbuf", [128, 256], "bfloat16"), "D12": ("sbuf", [128, 256], "bfloat16"),
     "Dr": ("sbuf", [128, 2048], "float16"), "ND": ("sbuf", [128, 512], "float16"), "LT": ("sbuf", [128, 512], "float16"),
     "nE": ("sbuf", [128, 16], "float32"), "negE": ("sbuf", [128, 16], "float32"),
-    "seg": ("sbuf", [128, 256], "bfloat16"), "RL1": ("sbuf", [128, 16], "uint16"), "RL2": ("sbuf", [128, 16], "uint16"),
+    "seg": ("sbuf", [128, 1024], "bfloat16"),
+    "RL1": ("sbuf", [128, 16], "uint16"), "RL2": ("sbuf", [128, 16], "uint16"),
     "RL3": ("sbuf", [128, 16], "uint16"), "i1": ("sbuf", [128, 16], "int32"), "i2": ("sbuf", [128, 16], "int32"),
     "i3": ("sbuf", [128, 16], "int32"), "pm": ("sbuf", [128, 16], "int32"), "pmf": ("sbuf", [128, 16], "float32"),
     "dq": ("sbuf", [128, 16], "float32"), "dum": ("sbuf", [128, 16], "float32"), "basec": ("sbuf", [128, 1], "float32"),
     "m16": ("sbuf", [128, 16], "bfloat16"), "mk4": ("sbuf", [128, 16], "float32"),
-    "offs": ("sbuf", [128, 16], "uint16"), "yo": ("sbuf", [128, 1], "int32"), "ya": ("sbuf", [128, 1], "int32"),
+    "offs": ("sbuf", [128, 16], "uint16"), "yo": ("sbuf", [128, 2], "int32"),
     "ca": ("sbuf", [128, 17], "float32"), "cb": ("sbuf", [128, 17], "float32"), "c1": ("sbuf", [128, 16], "float32"),
     "cE": ("sbuf", [128, 256], "float16"), "crow": ("sbuf", [128, 512], "float16"),
     "kc": ("sbuf", [128, 256], "uint16"), "kcq": ("sbuf", [128, 256], "uint16"), "kc16": ("sbuf", [128, 256], "float16"),
@@ -143,6 +145,9 @@ def rank_program(g, core, T, topo):
         else:
             op("v", lambda e: e.tensor_scalar(out, a, s1, s2, o0, o1), r, w, bk)
 
+    def scan(out, a, b, o0, o1, r, w, bk=()):
+        op("v", lambda e: e.tensor_tensor_scan(out, a, b, 0.0, o0, o1), r, w, bk)
+
     def act(out, in_, f, r, w, bk=(), bias=0.0, scale=1.0):
         op("s", lambda e: e.activation(out, in_, f, bias=bias, scale=scale), r, w, bk)
 
@@ -163,9 +168,9 @@ def rank_program(g, core, T, topo):
         gg, h = k // 2, k % 2
         dma("y" if h == 0 else "s", "dsl", T.T0[:, 128 * h + 16 * gg:128 * h + 16 * gg + 16],
             T.slips[16 * gg + 8 * h:16 * gg + 8 * h + 8, :], w=("T0_%d" % k,))
+    dma("y", "dr", T.recb[:], T.rec[:, :], w=("recb",))
     dma("y", "dk", T.Kw[:, 0:W], T.kin[:, :], w=("Kw",))
-    dma("s", "dr", T.recb[:], T.rec[:, :], w=("recb",))
-    dma("s", "dx", T.Xw[:], T.wealth[:, :], w=("Xw",))
+    dma("y", "dx", T.Xw[:], T.wealth[:, :], w=("Xw",))
 
     fill(T.ones[:], 1.0, ("ones",))
     sel(T.Ib[:], T.ones[:, 0:128], [[-1, 128]], A.is_equal, 0, 1, ("ones",), ("Ib",))
@@ -182,7 +187,7 @@ def rank_program(g, core, T, topo):
     op("g", lambda e: e.iota(T.Cm[:], [[0, 16], [-1, 16]], 15, 0, allow_small_or_imprecise_dtypes=True), (), ("Cm",))
 
     fill(T.seg[:], 1.0, ("seg",))
-    fill(T.seg[:, 0:256:16], 0.0, ("seg",))
+    fill(T.seg[:, 0:1024:16], 0.0, ("seg",))
     fill(T.m16[:], -16.0, ("m16",))
     fill(T.mk4[:], 4096.0, ("mk4",))
     fill(T.NT[:], 1.0, ("NT",))
@@ -202,17 +207,19 @@ def rank_program(g, core, T, topo):
     for h in range(2):
         mm(T.P2[:, 128 * h:128 * h + 128], T.T0h[:, 128 * h:128 * h + 128], T.I16[:], True, True, ("T0h", "I16"), ("pT0",), ("P2",))
     for h in range(2):
-        cp("v", T.SLd[:, 256 * h:256 * h + 256], T.P2[:, 0:256], ("pT0",), ("SLd",), ("P2",))
+        cp("v", T.SLd[:, 256 * h:256 * h + 256], T.P2[:, 0:256], ("pT0",), ("SLd%d" % h,), ("P2",))
     for r in range(16):
-        mm(T.P3[:, 0:16], T.Dr[:, 128 * r:128 * r + 128], T.SLd[:, 16 * r:16 * r + 16], r == 0, r == 15, ("Dr", "SLd"), ("pc0",), ("P3",))
+        mm(T.P3[:, 0:16], T.Dr[:, 128 * r:128 * r + 128], T.SLd[:, 16 * r:16 * r + 16], r == 0, r == 15, ("Dr", "SLd0"), ("pc0",), ("P3",))
     cp("v", T.cu0[:], T.P3[:, 0:16], ("pc0",), ("cu0",), ("P3",))
     send(T.rcv0[:], T.cu0[:], "rl0", T.cores[(rank + 1) % 6], ("cu0",))
     cp("v", T.ca[:, 1:17], T.P3[:, 0:16], ("pc0",), ("ca",), ("P3",))
-    act(T.Vw[:, 0:W], T.recb[:], F.Exp, ("recb",), ("Vw",), bias=0.0, scale=6.0 * math.log(2.0))
+    act(T.Vw[:, 0:W], T.recb[:], F.Exp, ("recb",), ("Vw",), scale=6.0 * math.log(2.0))
     mm(T.P1[:, 0:128], T.L8[0:8, :], T.L8[0:8, :], True, True, ("L8",), ("pB",), ("P1",))
     mm(T.P1[:, 128:272], T.L8[0:8, :], T.Z8[0:8, :], True, True, ("L8", "Z8"), ("pB",), ("P1",))
     mm(T.P1[:, 272:280], T.L8[0:8, :], T.G88[0:8, :], True, True, ("L8", "G88"), ("pB",), ("P1",))
     mm(T.P0[:, 256:512], T.L16[0:16, :], T.R16b[0:16, :], True, True, ("L16", "R16b"), ("pD",), ("P0",))
+    for r in range(16):
+        mm(T.P5[:, 0:256], T.Dr[:, 128 * r:128 * r + 128], T.SLd[:, 16 * r:16 * r + 256], r == 0, r == 15, ("Dr", "SLd0", "SLd1"), ("pSL",), ("P5",))
 
     def setup_vector():
         ts(T.pm[:], T.i1[:], 15, None, A.bitwise_and, None, ("i1",), ("pm",))
@@ -226,6 +233,7 @@ def rank_program(g, core, T, topo):
         ts(T.Gs[:], T.P1[:, 272:280], 16.0, None, A.mult, None, ("pB",), ("Gs",), ("P1",))
         cp("v", T.G16[:], T.P1[:, 272:280], ("pB",), ("G16",), ("P1",))
         cp("v", T.Zw[:], T.P1[:, 128:272], ("pB",), ("Zw",), ("P1",))
+        cp("v", T.Dm[:], T.P0[:, 256:512], ("pD",), ("Dm",), ("P0",))
         ts(T.NDH[:], T.P0[:, 256:512], -1e29, 1e29, A.mult, A.add, ("pD",), ("NDH",), ("P0",))
         ts(T.dum[:], T.dq[:], T.pmf[:, 0:1], None, A.add, None, ("dq", "pmf"), ("dum",))
         ts(T.basec[:], T.pmf[:, 0:1], 2048.0, None, A.add, None, ("pmf",), ("basec",))
@@ -237,11 +245,14 @@ def rank_program(g, core, T, topo):
             ts(T.ND[:, 128 * t:128 * t + 128], T.I16[:], T.nE[:, t:t + 1], None, A.mult, None, ("I16", "nE"), ("ND",))
         cp("v", T.TR16[:], T.TRb[:], ("TRb",), ("TR16",))
 
+    def bar_of_own_office(t):
+        act(T.DTH[:, 256 * t:256 * t + 256], T.NDH[:], F.Copy, ("NDH",), ("DTH%d" % t,), bias=2.0 ** (6 * (8 + t - 3)))
+
     def setup_scalar():
         for t in range(4):
-            act(T.DT[:, 256 * t:256 * t + 256], T.P0[:, 256:512], F.Copy, ("pD",), ("DT",), ("P0",), scale=2.0 ** (6 * (8 + t)))
+            act(T.DT[:, 256 * t:256 * t + 256], T.Dm[:], F.Copy, ("Dm",), ("DT%d" % t,), scale=2.0 ** (6 * (8 + t)))
         for t, n in ((11, "D11"), (12, "D12")):
-            act(T[n][:], T.P0[:, 256:512], F.Copy, ("pD",), (n,), ("P0",), scale=float(t))
+            act(T[n][:], T.Dm[:], F.Copy, ("Dm",), (n,), scale=float(t))
 
     for t in range(NR):
         last = t == NR - 1
@@ -250,26 +261,100 @@ def rank_program(g, core, T, topo):
         c, cprev = C[:, 1:17], C[:, 0:16]
         cu, rcv, scl = T["cu%d" % t], T["rcv%d" % t], T["scl%d" % t]
         cuk, rcvk, sclk = "cu%d" % t, "rcv%d" % t, "scl%d" % t
-        q = T.cores[(rank + 1 + t % 5) % 6]
         p = T.cores[(rank - 1 - t % 5) % 6]
+        rep, repk = T["rep%d" % t], "rep%d" % t
         lastw[rcvk] = ("rl%d" % t, 8)
         lastw["rrv%d" % t] = ("rr%d" % t, 8)
+        KB = ("P2", "P7")
+        eqpos = [256]
+        for b in range(15):
+            eqpos.append(eqpos[b] + 16 * (15 - b))
 
+        def ask(k):
+            a, b = ASK[k]
+            cp("v" if k in ASKV else "s", T.Vq[:, 16 * a:16 * b], T.Vw[:, 0:W].indirect(T.kcq[:, a:b]), ("Vw", "kcq"), ("Vq%d" % k,))
+
+        def ask_mm(k):
+            a, b = ASK[k]
+            for m in range(16):
+                mm(T.P1[:, a:b], T.Ib[:], T.Vq[:, 16 * a + m:16 * b:16], m == 0, m == 15, ("Ib", "Vq%d" % k), ("pA%d" % k,), ("P1",))
+
+        def own(k):
+            a, b = OWN[k]
+            cp("s", T.Vg[:, 16 * a:16 * b], T.Vw[:, 0:W].indirect(T.kc[:, a:b]), ("Vw", "kc"), ("Vg%d" % k,))
+
+        def own_mm(k):
+            a, b = OWN[k]
+            for m in range(16):
+                mm(T.P0[:, a:b], T.Ib[:], T.Vg[:, 16 * a + m:16 * b:16], False, False, ("Ib", "Vg%d" % k), ("pS",), ("P0",))
+
+        def wealth(h):
+            tt(T.Dx[:, 2048 * h:2048 * h + 2048], T.Xw[:].indirect(T.kc[:, 128 * h:128 * h + 128]), T.XCr[:, 2048 * h:2048 * h + 2048],
+               A.max, ("Xw", "kc") + tuple("XCr%d" % m for m in range(16)), ("Dx%d" % h,))
+
+        def key(h, m=None):
+            if m is None:
+                return T.P2[:, 0:128] if h == 0 else T.P7[:, 0:128]
+            return T.P2[:, m:128:16] if h == 0 else T.P7[:, m:128:16]
+
+        def score_mm(h):
+            mm(key(h), T.Ib[:], T.Cm[:, 128 * h:128 * h + 128], True, False, ("Ib", "Cm"), ("pKey%d" % h,), (KB[h],))
+            for m in range(16):
+                mm(key(h, m), T.Dx[:, 2048 * h + m:2048 * h + 2048:16], T.Gs[:], False, m == 15,
+                   ("Dx%d" % h, "Gs"), ("pKey%d" % h,), (KB[h],))
+
+        def eq_v():
+            for b in range(15):
+                ts(T.EQ[:, eqpos[b]:eqpos[b + 1]], T.crow[:, 16 * b + 16:256], T.c1[:, b:b + 1], None, A.is_equal, None, ("crow", "c1"), ("EQ%d" % b,))
+
+        def eq_mm():
+            for b in range(15):
+                mm(T.P5[:, 16 * b + 16:256], T.BOb[:], T.EQ[:, eqpos[b]:eqpos[b + 1]], False, b == 14, ("BOb", "EQ%d" % b), ("pcnt",), ("P5",))
+
+        def best_a(h):
+            a, b = 128 * h, 128 * h + 128
+            scan(T.y[:, a:b], T.seg[:, 0:128], key(h), A.mult, A.max, ("seg", "pKey%d" % h), ("y%d" % h,), (KB[h],))
+            tt(T.eqn[:, a:b], key(h), T.y[:, a:b], A.is_equal, ("pKey%d" % h, "y%d" % h), ("eqn%d" % h,), (KB[h],))
+            tt(T.neq[:, a:b], key(h), T.y[:, a:b], A.not_equal, ("pKey%d" % h, "y%d" % h), ("neq%d" % h,), (KB[h],))
+
+        def best_b(h):
+            a, b = 128 * h, 128 * h + 128
+            tt(T.ek[:, a:b], T.P3[:, a:b], T.eqn[:, a:b], A.mult, ("pkc", "eqn%d" % h), ("ek%d" % h,), ("P3",))
+            scan(T.s2[:, a:b], T.neq[:, a:b], T.ek[:, a:b], A.mult, A.add, ("neq%d" % h, "ek%d" % h), ("s2_%d" % h,))
+
+        def best_c(h):
+            a, b = 128 * h, 128 * h + 128
+            tt(T.Bx[:, a:b], T.s2[:, a:b].indirect(T.RL2[:, 0:8]), T.E[:, a:b], A.mult, ("s2_%d" % h, "RL2", "E"), ("Bx%d" % h,))
+
+        def best_mm(h):
+            mm(T.P4[:, 8 * h:8 * h + 8], T.Bx[:, 128 * h:128 * h + 128], T.G16[:], True, True, ("Bx%d" % h, "G16"), ("pBest",), ("P4",))
+
+        if t == 0:
+            setup_vector()
         cp("v", T.kc[:], T.Kw[:, 0:W].indirect(cu[:]), ("Kw", cuk), ("kc",))
         if t > 0:
-            ts_ = t - 1
-            pcl = T["scl%d" % ts_]
-            tt(T.Vw[:].indirect(pcl[:]), T.VC[:], T.DT[:, 256 * ts_:256 * ts_ + 256], A.add, ("VC", "DT", "scl%d" % ts_), ("Vw",))
-        else:
-            setup_vector()
+            tt(T.Vw[:].indirect(T["scl%d" % (t - 1)][:]), T.VC[:], T.DT[:, 256 * (t - 1):256 * t], A.add, ("VC", "DT%d" % (t - 1), "scl%d" % (t - 1)), ("Vw",))
+        if last:
+            cp("v", T.SL[:].indirect(T.offs[:, 2 * t:2 * t + 1]), T.mk4[:], ("mk4", "off%d" % t, cn, cuk), ("SL",))
+            for h in range(2):
+                cp("v", T.SLd[:, 256 * h:256 * h + 256], T.SL[:], ("SL",), ("SLd%d" % h,))
+            for r in range(16):
+                x = 16 * ((16 - r) % 16)
+                mm(T.P6[:, 256:512], T.Dr[:, 128 * r:128 * r + 128], T.SLd[:, x:x + 256], r == 0, r == 15, ("Dr", "SLd0", "SLd1"), ("pSU",), ("P6",))
         cp("s", T.XC[:], T.Xw[:].indirect(cu[:]), ("Xw", cuk), ("XC",))
         for m in range(NS):
             cp("s", T.XCr[:, m:4096:16], T.XC[:], ("XC",), ("XCr%d" % m,))
         cp("s", T.VC[:], T.Vw[:, 0:W].indirect(cu[:]), ("Vw", cuk), ("VC",))
-        cp("v", T.kcq[:], T.Kw[:, 0:W].indirect(rcv[:]), ("Kw", rcvk), ("kcq",))
         ts(T.c1[:], c, 1.0, None, A.add, None, (cn,), ("c1",))
         cp("v", T.kc16[:], T.kc[:], ("kc",), ("kc16",))
         tt(T.cE[:], T.c1[:].indirect(T.RL1[:]), T.E[:], A.mult, ("c1", "RL1", "E"), ("cE",))
+        for m in range(NS, 16):
+            cp("v", T.XCr[:, m:4096:16], T.XC[:], ("XC",), ("XCr%d" % m,))
+        cp("v", T.kcq[:], T.Kw[:, 0:W].indirect(rcv[:]), ("Kw", rcvk), ("kcq",))
+        for k in range(PRE):
+            own(k)
+        for k in ASKO:
+            ask(k)
         mm(T.P4[:, 0:256], T.BO16[:], T.cE[:], True, True, ("BO16", "cE"), ("pcrow",), ("P4",))
         mm(T.P4[:, 256:512], T.TR16[:], T.cE[:], True, True, ("TR16", "cE"), ("pcrow",), ("P4",))
         for h in range(2):
@@ -278,118 +363,69 @@ def rank_program(g, core, T, topo):
             mm(T.P3[:, 256:512], T.ND[:, 128 * t:128 * t + 128], T.kc16[:], True, False, ("ND", "kc16"), ("pnK",), ("P3",))
             mm(T.P3[:, 256:512:2], T.LT[:, 128 * t:128 * t + 128], T.cE[:, 1:256:2], False, False, ("LTx", "cE"), ("pnK",), ("P3",))
             mm(T.P3[:, 257:512:2], T.LT[:, 128 * t:128 * t + 128], T.cE[:, 0:256:2], False, True, ("LTx", "cE"), ("pnK",), ("P3",))
-        for m in range(NS, 16):
-            cp("v", T.XCr[:, m:4096:16], T.XC[:], ("XC",), ("XCr%d" % m,))
-        cp("v", T.crow[:], T.P4[:], ("pcrow",), ("crow",), ("P4",))
         if last:
-            cp("v", T.SL[:].indirect(T.offs[:, 2 * t:2 * t + 1]), T.mk4[:], ("mk4", "off%d" % t, cn, cuk), ("SL",))
-            for h in range(2):
-                cp("v", T.SLd[:, 256 * h:256 * h + 256], T.SL[:], ("SL",), ("SLd",))
             ts(T.Rw[:, 0:W], T.r24[:], 16.0, None, A.subtract, None, ("r24",), ("Rw",))
+            tt(T.nR[:], T.Rw[:, 0:W].indirect(T.cu3[:]), T.D11[:], A.max, ("Rw", "cu3", "D11"), ("nR",))
 
         mm(T.P0[:, 0:256], T.Ib[:], T.VC[:], True, False, ("Ib", "VC"), ("pS",), ("P0",))
-        for k, (a, b) in enumerate(ASK):
-            cp("s", T.Vq[:, 16 * a:16 * b], T.Vw[:, 0:W].indirect(T.kcq[:, a:b]), ("Vw", "kcq"), ("Vq%d" % k,))
-            for m in range(16):
-                mm(T.P1[:, a:b], T.Ib[:], T.Vq[:, 16 * a + m:16 * b:16], m == 0, m == 15, ("Ib", "Vq%d" % k), ("pA",), ("P1",))
-        if t == 0:
-            for r in range(16):
-                mm(T.P5[:, 0:256], T.Dr[:, 128 * r:128 * r + 128], T.SLd[:, 16 * r:16 * r + 256], r == 0, r == 15, ("Dr", "SLd"), ("pSL",), ("P5",))
-
-        def own_mm(k, a, b):
-            for m in range(16):
-                mm(T.P0[:, a:b], T.Ib[:], T.Vg[:, 16 * a + m:16 * b:16], False, False, ("Ib", "Vg%d" % k), ("pS",), ("P0",))
-
-        def own_s(k):
-            a, b = OWN_S[k]
-            cp("s", T.Vg[:, 16 * a:16 * b], T.Vw[:, 0:W].indirect(T.kc[:, a:b]), ("Vw", "kc"), ("Vg%d" % k,))
-
-        def wealth_half(h):
-            tt(T.Dx[:, 2048 * h:2048 * h + 2048], T.Xw[:].indirect(T.kc[:, 128 * h:128 * h + 128]), T.XCr[:, 2048 * h:2048 * h + 2048],
-               A.max, ("Xw", "kc") + tuple("XCr%d" % m for m in range(16)), ("Dx%d" % h,))
-
-        def score_mm(h):
-            mm(T.P2[:, 128 * h:128 * h + 128], T.Ib[:], T.Cm[:, 128 * h:128 * h + 128], True, False, ("Ib", "Cm"), ("pKey",), ("P2",))
-            for m in range(16):
-                mm(T.P2[:, 128 * h + m:128 * h + 128:16], T.Dx[:, 2048 * h + m:2048 * h + 2048:16], T.Gs[:], False, m == 15,
-                   ("Dx%d" % h, "Gs"), ("pKey",), ("P2",))
-
-        eqo = [256]
-        eqpos = []
-        for b in range(15):
-            eqpos.append(eqo[0])
-            eqo[0] += 16 * (15 - b)
-
-        def eq_v(lo, hi):
-            for b in range(lo, hi):
-                n = 16 * (15 - b)
-                ts(T.EQ[:, eqpos[b]:eqpos[b] + n], T.crow[:, 16 * b + 16:256], T.c1[:, b:b + 1], None, A.is_equal, None, ("crow", "c1"), ("EQ%d" % b,))
-
-        def eq_mm(lo, hi):
-            for b in range(lo, hi):
-                n = 16 * (15 - b)
-                mm(T.P5[:, 16 * b + 16:256], T.BOb[:], T.EQ[:, eqpos[b]:eqpos[b] + n], False, b == 14, ("BOb", "EQ%d" % b), ("pcnt",), ("P5",))
-
-        own_s(0)
-        cp("s", T["rep%d" % t][:], T.P1[:, 0:256], ("pA",), ("rep%d" % t,), ("P1",))
-        send(T["rrv%d" % t][:], T["rep%d" % t][:], "rr%d" % t, p, ("rep%d" % t,))
-        own_s(1)
-        if t == 0:
-            setup_scalar()
-        act(T.DTH[:, 256 * t:256 * t + 256], T.NDH[:], F.Copy, ("NDH",), ("DTH%d" % t,), bias=2.0 ** (6 * (8 + t - 3)))
-        if not last:
-            act(T.nK[:], T.P3[:, 256:512], F.Identity, ("pnK", "negE"), ("nK",), ("P3",), bias=T.negE[:, t:t + 1])
-        own_s(2)
-        own_s(3)
-
-        wealth_half(0)
-        score_mm(0)
-        own_mm(0, *OWN_S[0])
+        for k in range(PRE):
+            own_mm(k)
+        for k in ASKO:
+            ask_mm(k)
+        for k in range(PRE, MID):
+            own(k)
+        cp("s", rep[:], T.P1[:, 0:256], tuple("pA%d" % k for k in ASKO), (repk,), ("P1",))
+        send(T["rrv%d" % t][:], rep[:], "rr%d" % t, p, (repk,))
+        wealth(0)
+        cp("v", T.crow[:], T.P4[:], ("pcrow",), ("crow",), ("P4",))
         tt(T.EQ[:, 0:256], T.c1[:].indirect(T.RL1[:]), T.crow[:, 256:512], A.is_equal, ("c1", "RL1", "crow"), ("EQin",))
+        eq_v()
+        score_mm(0)
         if t == 0:
             cp("v", T.SL[:], T.P5[:, 0:256], ("pSL",), ("SL",), ("P5",))
-        eq_v(0, 8)
         mm(T.P5[:, 0:256], T.BOb[:], T.EQ[:, 0:256], True, False, ("BOb", "EQin"), ("pcnt",), ("P5",))
-        eq_mm(0, 8)
-        own_mm(1, *OWN_S[1])
-        wealth_half(1)
-        if last:
-            for r in range(16):
-                x = 16 * ((16 - r) % 16)
-                mm(T.P7[:, 0:256], T.Dr[:, 128 * r:128 * r + 128], T.SLd[:, x:x + 256], r == 0, r == 15, ("Dr", "SLd"), ("pSU",), ("P7",))
-        own_mm(2, *OWN_S[2])
+        eq_mm()
+        for k in range(PRE, MID):
+            own_mm(k)
+        wealth(1)
+        own(MID)
+        own_mm(MID)
         score_mm(1)
-        eq_v(8, 15)
-        eq_mm(8, 15)
+        for k in range(MID + 1, len(OWN)):
+            own(k)
         act(T.UU[:, 512:768], T.P5[:, 0:256], F.Copy, ("pcnt",), ("UUn",), ("P5",), scale=4.0)
-        a, b = OWN_V
-        cp("v", T.Vg[:, 16 * a:16 * b], T.Vw[:, 0:W].indirect(T.kc[:, a:b]), ("Vw", "kc"), ("Vg4",))
-        own_mm(3, *OWN_S[3])
-        own_mm(4, a, b)
+        if not last:
+            bar_of_own_office(t + 1)
+        if t == 0:
+            bar_of_own_office(0)
+        best_a(0)
+        best_b(0)
+        best_c(0)
+        for k in range(MID + 1, len(OWN)):
+            own_mm(k)
         if t == 3:
             act(T.lnb[:], T.Vw[:, 0:W], F.Ln, ("Vw",), ("lnb",), scale=2.0 ** -48)
             act(T.r24[:], T.lnb[:], F.Copy, ("lnb",), ("r24",), scale=1.0 / (6.0 * math.log(2.0)), bias=24.0)
         if last:
-            tt(T.nR[:], T.Rw[:, 0:W].indirect(T.cu3[:]), T.D11[:], A.max, ("Rw", "cu3", "D11"), ("nR",))
             cp("v", T.Rw[:].indirect(T.scl3[:]), T.nR[:], ("nR", "scl3", "Rw"), ("Rw",))
             tt(T.nR[:], T.Rw[:, 0:W].indirect(cu[:]), T.D12[:], A.max, ("Rw", cuk, "D12"), ("nR",))
-            ts(T.msk[:], T.P7[:, 0:256], 4096.0, None, A.is_ge, None, ("pSU",), ("msk",), ("P7",))
-            ts(T.ltm[:], T.P7[:, 0:256], 4096.0, None, A.is_lt, None, ("pSU",), ("ltm",), ("P7",))
-        op("v", lambda e: e.tensor_tensor_scan(T.y[:], T.seg[:], T.P2[:, 0:256], 0.0, A.mult, A.max), ("seg", "pKey"), ("y",), ("P2",))
-        if last:
-            tt(T.SLz[:], T.P7[:, 0:256], T.ltm[:], A.mult, ("pSU", "ltm"), ("SLz",), ("P7",))
-        tt(T.eqn[:], T.P2[:, 0:256], T.y[:], A.is_equal, ("pKey", "y"), ("eqn",), ("P2",))
-        tt(T.neq[:], T.P2[:, 0:256], T.y[:], A.not_equal, ("pKey", "y"), ("neq",), ("P2",))
-        tt(T.ek[:], T.P3[:, 0:256], T.eqn[:], A.mult, ("pkc", "eqn"), ("ek",), ("P3",))
-        op("v", lambda e: e.tensor_tensor_scan(T.s2[:], T.neq[:], T.ek[:], 0.0, A.mult, A.add), ("neq", "ek"), ("s2",))
-        tt(T.Bx[:], T.s2[:].indirect(T.RL2[:]), T.E[:], A.mult, ("s2", "RL2", "E"), ("Bx",))
-        for h in range(2):
-            mm(T.P7[:, 256 + 8 * h:264 + 8 * h], T.Bx[:, 128 * h:128 * h + 128], T.G16[:], True, True, ("Bx", "G16"), ("pBest",), ("P7",))
+            ts(T.msk[:], T.P6[:, 256:512], 4096.0, None, A.is_ge, None, ("pSU",), ("msk",), ("P6",))
+            ts(T.ltm[:], T.P6[:, 256:512], 4096.0, None, A.is_lt, None, ("pSU",), ("ltm",), ("P6",))
+            tt(T.SLz[:], T.P6[:, 256:512], T.ltm[:], A.mult, ("pSU", "ltm"), ("SLz",), ("P6",))
+        best_a(1)
         mm(T.P0[:, 0:256], T.Ib[:], T["rrv%d" % t][:], False, True, ("Ib", "rrv%d" % t), ("pS",), ("P0",))
         ts(T.UU[:, 0:256], T.P0[:, 0:256], 2.0 ** (6 * (8 + t - 2)), None, A.is_ge, None, ("pS",), ("UU2",), ("P0",))
         tt(T.UU[:, 256:512], T.P0[:, 0:256], T.DTH[:, 256 * t:256 * t + 256], A.is_ge, ("pS", "DTH%d" % t), ("UU3",), ("P0",))
         for j in range(16):
             mm(T.P6[:, 0:48], T.Zw[:, 15 - j:143 - j], T.UU[:, j:768:16], j == 0, j == 15, ("Zw", "UU2", "UU3", "UUn"), ("pF",), ("P6",))
+        best_b(1)
+        if not last:
+            act(T.nK[:], T.P3[:, 256:512], F.Identity, ("pnK", "negE"), ("nK",), ("P3",), bias=T.negE[:, t:t + 1])
+        if t == 0:
+            setup_scalar()
+        best_c(1)
+        best_mm(0)
+        best_mm(1)
         cp("v", T.Bf[:], T.P6[:, 0:48], ("pF",), ("Bf",), ("P6",))
         sm = [T.sm[:, 16 * k:16 * k + 16] for k in range(16)]
         tt(T.wi[:], T.Bf[:, 0:16], T.Bf[:, 32:48], A.add, ("Bf",), ("wi",))
@@ -414,18 +450,18 @@ def rank_program(g, core, T, topo):
             cp("v", T.Rw[:].indirect(scl[:]), T.nR[:], ("nR", sclk, "Rw"), ("Rw",))
             dma("y", "dout", T.yr[:, :], T.Rw[:, 0:W], r=("Rw",))
         else:
-            ts(T.yo[:], T.P6[:, 64:65], T.basec[:, 0:1], float(16 * (t + 1)), A.add, A.add, ("pOff", "basec"), ("yo",), ("P6",))
+            ts(T.yo[:, 0:1], T.P6[:, 64:65], T.basec[:, 0:1], float(16 * (t + 1)), A.add, A.add, ("pOff", "basec"), ("yo",), ("P6",))
         tt(sm[9], T.NT[:, 0:16], T.mv[:, 1:17], A.is_gt, ("NT", "mv"), ("NM",))
         tt(sm[11], T.mv[:, 0:16], cprev, A.mult, ("mv", cn), ("R2",))
         if not last:
-            ts(T.ya[:], T.yo[:], 255, None, A.bitwise_and, None, ("yo",), ("ya",))
+            ts(T.yo[:, 1:2], T.yo[:, 0:1], 255, None, A.bitwise_and, None, ("yo",), ("ya",))
         tt(sm[10], sm[9], c, A.mult, ("NM", cn), ("R1",))
         tt(sm[12], sm[9], T.mv[:, 0:16], A.add, ("NM", "mv"), ("q1",))
         tt(sm[13], sm[10], sm[11], A.add, ("R1", "R2"), ("R12",))
         ts(sm[14], sm[12], -1.0, 1.0, A.mult, A.add, ("q1",), ("Bm",))
         if not last:
-            cp("v", T.offs[:, 2 * t + 2:2 * t + 3], T.ya[:], ("ya",), ("off%d" % (t + 1),))
-        tt(sm[15], T.P7[:, 256:272], sm[14], A.mult, ("pBest", "Bm"), ("xb",), ("P7",))
+            cp("v", T.offs[:, 2 * t + 2:2 * t + 3], T.yo[:, 1:2], ("ya",), ("off%d" % (t + 1),))
+        tt(sm[15], T.P4[:, 0:16], sm[14], A.mult, ("pBest", "Bm"), ("xb",), ("P4",))
         tt(T.nw[:], sm[15], sm[13], A.add, ("xb", "R12"), ("nw",))
         if not last:
             cp("v", T.SL[:].indirect(T.offs[:, 2 * t:2 * t + 1]), T.nw[:], ("nw", "off%d" % t, "SL"), ("SL",))
@@ -438,9 +474,10 @@ def rank_program(g, core, T, topo):
         else:
             tt(T.nm[:], T.nw[:].indirect(T.RL3[:]), T.msk[:], A.mult, ("nw", "RL3", "msk"), ("nm",))
             for h in range(2):
-                mm(T.P4[:, 128 * h:128 * h + 128], T.SLz[:, 128 * h:128 * h + 128], T.I16[:], True, False, ("SLz", "I16"), ("pY",), ("P4",))
-                mm(T.P4[:, 128 * h:128 * h + 128], T.nm[:, 128 * h:128 * h + 128], T.I16[:], False, True, ("nm", "I16"), ("pY",), ("P4",))
-            cp("v", T.ysb[:], T.P4[:, 0:256], ("pY",), ("ysb",), ("P4",))
+                a, b = 256 + 128 * h, 384 + 128 * h
+                mm(T.P4[:, a:b], T.SLz[:, 128 * h:128 * h + 128], T.I16[:], True, False, ("SLz", "I16"), ("pY",), ("P4",))
+                mm(T.P4[:, a:b], T.nm[:, 128 * h:128 * h + 128], T.I16[:], False, True, ("nm", "I16"), ("pY",), ("P4",))
+            cp("v", T.ysb[:], T.P4[:, 256:512], ("pY",), ("ysb",), ("P4",))
             for k in range(16):
                 gg, h = k // 2, k % 2
                 dma("y" if h == 0 else "s", "dout", T.ys[16 * gg + 8 * h:16 * gg + 8 * h + 8, :],

import numpy as np
import math
from concourse.mybir import dt, AluOpType, AxisListType, ActivationFunctionType

W, NR = 1408, 5
WD = W + 256
NS = 10
OWN = ((0, 32), (32, 64), (64, 128), (128, 192), (192, 256))
PRE, MID = 1, 2
ASK = ((0, 96), (96, 160), (160, 192), (192, 256))
ASKV, ASKO = (3,), (3, 0, 1, 2)

SCRATCH = {
    "Kw": ("sbuf", [128, WD], "int32"), "Vw": ("sbuf", [128, WD], "bfloat16"), "Rw": ("sbuf", [128, WD], "bfloat16"),
    "Xw": ("sbuf", [128, W], "bfloat16"), "recb": ("sbuf", [128, W], "bfloat16"),
    "lnb": ("sbuf", [128, W], "float32"), "r24": ("sbuf", [128, W], "bfloat16"),
    "T0": ("sbuf", [128, 256], "int32"), "T0h": ("sbuf", [128, 256], "float16"), "SLd": ("sbuf", [128, 512], "float16"),
    "SL": ("sbuf", [128, 256], "float32"),
    "ones": ("sbuf", [128, 256], "bfloat16"), "L16": ("sbuf", [128, 128], "bfloat16"), "R16b": ("sbuf", [128, 256], "bfloat16"),
    "R16j": ("sbuf", [128, 256], "bfloat16"), "L8": ("sbuf", [128, 128], "bfloat16"), "Z8": ("sbuf", [128, 144], "bfloat16"),
    "G88": ("sbuf", [128, 8], "bfloat16"), "Ib": ("sbuf", [128, 128], "bfloat16"), "I16": ("sbuf", [128, 128], "float16"),
    "E": ("sbuf", [128, 256], "bfloat16"), "BOb": ("sbuf", [128, 128], "bfloat16"), "BO16": ("sbuf", [128, 128], "float16"),
    "TRb": ("sbuf", [128, 128], "bfloat16"), "TR16": ("sbuf", [128, 128], "float16"), "Zw": ("sbuf", [128, 144], "bfloat16"),
    "Gs": ("sbuf", [128, 8], "bfloat16"), "G16": ("sbuf", [128, 8], "float16"), "Cm": ("sbuf", [128, 256], "bfloat16"),
    "Dm": ("sbuf", [128, 256], "bfloat16"), "NDH": ("sbuf", [128, 256], "float32"), "DT": ("sbuf", [128, 1024], "bfloat16"), "DTH": ("sbuf", [128, 1280], "float32"),
    "D11": ("sbuf", [128, 256], "bfloat16"), "D12": ("sbuf", [128, 256], "bfloat16"),
    "Dr": ("sbuf", [128, 2048], "float16"), "ND": ("sbuf", [128, 512], "float16"), "LT": ("sbuf", [128, 512], "float16"),
    "nE": ("sbuf", [128, 16], "float32"), "negE": ("sbuf", [128, 16], "float32"),
    "seg": ("sbuf", [128, 1024], "bfloat16"),
    "RL1": ("sbuf", [128, 16], "uint16"), "RL2": ("sbuf", [128, 16], "uint16"),
    "RL3": ("sbuf", [128, 16], "uint16"), "i1": ("sbuf", [128, 16], "int32"), "i2": ("sbuf", [128, 16], "int32"),
    "i3": ("sbuf", [128, 16], "int32"), "pm": ("sbuf", [128, 16], "int32"), "pmf": ("sbuf", [128, 16], "float32"),
    "dq": ("sbuf", [128, 16], "float32"), "dum": ("sbuf", [128, 16], "float32"), "basec": ("sbuf", [128, 1], "float32"),
    "m16": ("sbuf", [128, 16], "bfloat16"), "mk4": ("sbuf", [128, 16], "float32"),
    "offs": ("sbuf", [128, 16], "uint16"), "yo": ("sbuf", [128, 2], "int32"),
    "ca": ("sbuf", [128, 17], "float32"), "cb": ("sbuf", [128, 17], "float32"), "c1": ("sbuf", [128, 16], "float32"),
    "cE": ("sbuf", [128, 256], "float16"), "crow": ("sbuf", [128, 512], "float16"),
    "kc": ("sbuf", [128, 256], "uint16"), "kcq": ("sbuf", [128, 256], "uint16"), "kc16": ("sbuf", [128, 256], "float16"),
    "XC": ("sbuf", [128, 256], "bfloat16"), "XCr": ("sbuf", [128, 4096], "bfloat16"), "VC": ("sbuf", [128, 256], "bfloat16"),
    "Vg": ("sbuf", [128, 4096], "bfloat16"), "Vq": ("sbuf", [128, 4096], "bfloat16"), "Dx": ("sbuf", [128, 4096], "bfloat16"),
    "EQ": ("sbuf", [128, 2176], "bfloat16"), "UU": ("sbuf", [128, 768], "bfloat16"), "nK": ("sbuf", [128, 256], "float32"),
    "nR": ("sbuf", [128, 256], "bfloat16"),
    "y": ("sbuf", [128, 256], "float32"), "eqn": ("sbuf", [128, 256], "bfloat16"), "neq": ("sbuf", [128, 256], "bfloat16"),
    "ek": ("sbuf", [128, 256], "float32"), "s2": ("sbuf", [128, 256], "float32"), "Bx": ("sbuf", [128, 256], "float16"),
    "Bf": ("sbuf", [128, 48], "float32"), "sm": ("sbuf", [128, 256], "float32"), "gq": ("sbuf", [128, 16], "float32"),
    "wi": ("sbuf", [128, 16], "int32"), "pp": ("sbuf", [128, 16], "int32"), "nirep": ("sbuf", [128, 128], "bfloat16"),
    "NT": ("sbuf", [128, 17], "float32"), "mv": ("sbuf", [128, 17], "float32"), "nw": ("sbuf", [128, 16], "float32"),
    "msk": ("sbuf", [128, 256], "float16"), "ltm": ("sbuf", [128, 256], "float16"), "SLz": ("sbuf", [128, 256], "float16"),
    "nm": ("sbuf", [128, 256], "float16"), "ysb": ("sbuf", [128, 256], "float32"),
}
for _t in range(NR):
    SCRATCH["cu%d" % _t] = ("sbuf", [128, 16], "uint16")
    SCRATCH["rcv%d" % _t] = ("sbuf", [128, 16], "uint16")
    SCRATCH["rep%d" % _t] = ("sbuf", [128, 256], "bfloat16")
    SCRATCH["rrv%d" % _t] = ("sbuf", [128, 256], "bfloat16")
    SCRATCH["scl%d" % _t] = ("sbuf", [128, 16], "uint16")
for _k in range(8):
    SCRATCH["P%d" % _k] = ("psum", [128, 512], "float32")
SEMAPHORES = ["v", "s", "t", "g", "dsl", "dk", "dr", "dx", "loc", "dout"] + ["rl%d" % t for t in range(NR)] + ["rr%d" % t for t in range(NR)]


def rank_program(g, core, T, topo):
    rank = T.rank_of(core)
    if rank is None:
        return
    A, F = AluOpType, ActivationFunctionType
    queues = {"v": g.vector, "s": g.scalar, "t": g.tensor, "g": g, "y": g.sync}
    cnt = {}
    seen = {q: {} for q in queues}
    snap = {}
    lastw, readers, bank = {}, {}, {}

    def wait(q, tok):
        sem, val = tok
        if seen[q].get(sem, 0) >= val:
            return
        queues[q].wait_ge(T.sem[sem], val)
        seen[q][sem] = val
        for s, x in snap.get(tok, {}).items():
            if seen[q].get(s, 0) < x:
                seen[q][s] = x

    def deps(q, r, w, bk):
        need = {}

        def add(tok):
            if tok is not None and need.get(tok[0], 0) < tok[1]:
                need[tok[0]] = tok[1]
        for k in r:
            tok = lastw.get(k)
            if tok is not None and not (q == "t" and tok[0] == "t"):
                add(tok)
        for k in w:
            tok = lastw.get(k)
            if tok is not None and not (q == "t" and tok[0] == "t"):
                add(tok)
            for x, tok in readers.get(k, {}).items():
                if x != q:
                    add(tok)
        for b in bk:
            for x, tok in bank.get(b, {}).items():
                if x != q:
                    add(tok)
        for s in sorted(need):
            wait(q, (s, need[s]))

    def note(q, tok, r, w, bk):
        snap[tok] = dict(seen[q])
        for k in r:
            readers.setdefault(k, {})[q] = tok
        for k in w:
            lastw[k] = tok
            readers[k] = {}
        for b in bk:
            bank.setdefault(b, {})[q] = tok

    def op(q, fn, r=(), w=(), bk=()):
        deps(q, r, w, bk)
        fn(queues[q]).then_inc(T.sem[q], 1)
        cnt[q] = cnt.get(q, 0) + 1
        note(q, (q, cnt[q]), r, w, bk)

    def dma(q, sem, out, in_, r=(), w=()):
        deps(q, r, w, ())
        queues[q].dma_start(out, in_).then_inc(T.sem[sem], 16)
        cnt[sem] = cnt.get(sem, 0) + 16
        for k in w:
            lastw[k] = (sem, cnt[sem])

    def mm(out, lhsT, rhs, start, stop, r=(), w=(), bk=()):
        op("t", lambda e: e.matmul(out, lhsT, rhs, start, stop), r, w, bk)

    def cp(q, out, in_, r, w, bk=()):
        if q == "s":
            op("s", lambda e: e.activation(out, in_, F.Copy), r, w, bk)
        else:
            op("v", lambda e: e.tensor_copy(out, in_), r, w, bk)

    def tt(out, a, b, o, r, w, bk=()):
        op("v", lambda e: e.tensor_tensor(out, a, b, o), r, w, bk)

    def ts(out, a, s1, s2, o0, o1, r, w, bk=()):
        if o1 is None:
            op("v", lambda e: e.tensor_scalar(out, a, s1, None, o0), r, w, bk)
        else:
            op("v", lambda e: e.tensor_scalar(out, a, s1, s2, o0, o1), r, w, bk)

    def scan(out, a, b, o0, o1, r, w, bk=()):
        op("v", lambda e: e.tensor_tensor_scan(out, a, b, 0.0, o0, o1), r, w, bk)

    def act(out, in_, f, r, w, bk=(), bias=0.0, scale=1.0):
        op("s", lambda e: e.activation(out, in_, f, bias=bias, scale=scale), r, w, bk)

    def fill(ap, val, w):
        op("v", lambda e: e.memset(ap, val), (), w)

    def sel(out, in_, pat, o, base, cm, r, w):
        op("g", lambda e: e.affine_select(out, in_, pat, o, 0.0, base, cm), r, w)

    def send(out, in_, rsem, dst, r):
        deps("g", r, (), ())
        eng = topo.engines(core, dst)[:8]
        rid, pid = topo.addr(dst, core)
        g.remote_dma(out, in_, T.sem[rsem], T.sem.loc, pid, rid, sum(1 << e for e in eng))
        cnt["loc"] = cnt.get("loc", 0) + len(eng)

    for k in range(16):
        gg, h = k // 2, k % 2
        dma("y" if h == 0 else "s", "dsl", T.T0[:, 128 * h + 16 * gg:128 * h + 16 * gg + 16],
            T.slips[16 * gg + 8 * h:16 * gg + 8 * h + 8, :], w=("T0_%d" % k,))
    dma("y", "dr", T.recb[:], T.rec[:, :], w=("recb",))
    dma("y", "dk", T.Kw[:, 0:W], T.kin[:, :], w=("Kw",))
    dma("y", "dx", T.Xw[:], T.wealth[:, :], w=("Xw",))

    fill(T.ones[:], 1.0, ("ones",))
    sel(T.Ib[:], T.ones[:, 0:128], [[-1, 128]], A.is_equal, 0, 1, ("ones",), ("Ib",))
    sel(T.L16[0:16, :], T.ones[0:16, 0:128], [[0, 8], [1, 16]], A.is_equal, 0, -1, ("ones",), ("L16",))
    sel(T.R16j[0:16, :], T.ones[0:16, :], [[0, 16], [1, 16]], A.is_equal, 0, -1, ("ones",), ("R16j",))
    op("g", lambda e: e.iota(T.i1[:], [[0, 16]], 0, 1), (), ("i1",))
    sel(T.L8[0:8, :], T.ones[0:8, 0:128], [[1, 8], [0, 16]], A.is_equal, 0, -1, ("ones",), ("L8",))
    op("g", lambda e: e.iota(T.i2[:], [[1, 16]], 0, 0), (), ("i2",))
    sel(T.R16b[0:16, :], T.ones[0:16, :], [[1, 16], [0, 16]], A.is_equal, 0, -1, ("ones",), ("R16b",))
    sel(T.Z8[0:8, :], T.ones[0:8, 0:144], [[1, 144]], A.is_equal, -15, -16, ("ones",), ("Z8",))
    sel(T.G88[0:8, :], T.ones[0:8, 0:8], [[1, 8]], A.is_equal, 0, -1, ("ones",), ("G88",))
    op("g", lambda e: e.iota(T.i3[:], [[16, 16]], 15, 0), (), ("i3",))
    op("g", lambda e: e.iota(T.dq[:], [[16, 16]], W, 0, allow_small_or_imprecise_dtypes=True), (), ("dq",))
    op("g", lambda e: e.iota(T.Cm[:], [[0, 16], [-1, 16]], 15, 0, allow_small_or_imprecise_dtypes=True), (), ("Cm",))

    fill(T.seg[:], 1.0, ("seg",))
    fill(T.seg[:, 0:1024:16], 0.0, ("seg",))
    fill(T.m16[:], -16.0, ("m16",))
    fill(T.mk4[:], 4096.0, ("mk4",))
    fill(T.NT[:], 1.0, ("NT",))
    fill(T.mv[:], 0.0, ("mv",))
    fill(T.ca[:], 0.0, ("ca",))
    fill(T.cb[:], 0.0, ("cb",))
    ts(T.LT[:, 0:256], T.ones[:], 0.0, None, A.mult, None, ("ones",), ("LT",))
    ts(T.LT[:, 256:512], T.ones[:], 0.0, None, A.mult, None, ("ones",), ("LT",))

    cp("v", T.I16[:], T.Ib[:], ("Ib",), ("I16",))
    mm(T.P0[:, 0:256], T.L16[0:16, :], T.R16j[0:16, :], True, True, ("L16", "R16j"), ("pE",), ("P0",))
    cp("v", T.E[:], T.P0[:, 0:256], ("pE",), ("E",), ("P0",))
    for j in range(16):
        r = 5 * j % 16
        ts(T.Dr[:, 128 * r:128 * r + 128], T.I16[:], T.E[:, j:j + 1], None, A.mult, None, ("I16", "E"), ("Dr",))
    cp("v", T.T0h[:], T.T0[:], tuple("T0_%d" % k for k in range(16)), ("T0h",))
    for h in range(2):
        mm(T.P2[:, 128 * h:128 * h + 128], T.T0h[:, 128 * h:128 * h + 128], T.I16[:], True, True, ("T0h", "I16"), ("pT0",), ("P2",))
    for h in range(2):
        cp("v", T.SLd[:, 256 * h:256 * h + 256], T.P2[:, 0:256], ("pT0",), ("SLd%d" % h,), ("P2",))
    for r in range(16):
        mm(T.P3[:, 0:16], T.Dr[:, 128 * r:128 * r + 128], T.SLd[:, 16 * r:16 * r + 16], r == 0, r == 15, ("Dr", "SLd0"), ("pc0",), ("P3",))
    cp("v", T.cu0[:], T.P3[:, 0:16], ("pc0",), ("cu0",), ("P3",))
    send(T.rcv0[:], T.cu0[:], "rl0", T.cores[(rank + 1) % 6], ("cu0",))
    cp("v", T.ca[:, 1:17], T.P3[:, 0:16], ("pc0",), ("ca",), ("P3",))
    act(T.Vw[:, 0:W], T.recb[:], F.Exp, ("recb",), ("Vw",), scale=6.0 * math.log(2.0))
    mm(T.P1[:, 0:128], T.L8[0:8, :], T.L8[0:8, :], True, True, ("L8",), ("pB",), ("P1",))
    mm(T.P1[:, 128:272], T.L8[0:8, :], T.Z8[0:8, :], True, True, ("L8", "Z8"), ("pB",), ("P1",))
    mm(T.P1[:, 272:280], T.L8[0:8, :], T.G88[0:8, :], True, True, ("L8", "G88"), ("pB",), ("P1",))
    mm(T.P0[:, 256:512], T.L16[0:16, :], T.R16b[0:16, :], True, True, ("L16", "R16b"), ("pD",), ("P0",))
    for r in range(16):
        mm(T.P5[:, 0:256], T.Dr[:, 128 * r:128 * r + 128], T.SLd[:, 16 * r:16 * r + 256], r == 0, r == 15, ("Dr", "SLd0", "SLd1"), ("pSL",), ("P5",))

    def setup_vector():
        ts(T.pm[:], T.i1[:], 15, None, A.bitwise_and, None, ("i1",), ("pm",))
        cp("v", T.RL1[:], T.i2[:], ("i2",), ("RL1",))
        cp("v", T.BO16[:], T.P1[:, 0:128], ("pB",), ("BO16",), ("P1",))
        cp("v", T.BOb[:], T.P1[:, 0:128], ("pB",), ("BOb",), ("P1",))
        sel(T.TRb[:], T.BOb[:], [[-1, 128]], A.is_gt, 0, 1, ("BOb",), ("TRb",))
        cp("v", T.RL3[:], T.pm[:], ("pm",), ("RL3",))
        cp("v", T.pmf[:], T.pm[:], ("pm",), ("pmf",))
        cp("v", T.RL2[:], T.i3[:], ("i3",), ("RL2",))
        ts(T.Gs[:], T.P1[:, 272:280], 16.0, None, A.mult, None, ("pB",), ("Gs",), ("P1",))
        cp("v", T.G16[:], T.P1[:, 272:280], ("pB",), ("G16",), ("P1",))
        cp("v", T.Zw[:], T.P1[:, 128:272], ("pB",), ("Zw",), ("P1",))
        cp("v", T.Dm[:], T.P0[:, 256:512], ("pD",), ("Dm",), ("P0",))
        ts(T.NDH[:], T.P0[:, 256:512], -1e29, 1e29, A.mult, A.add, ("pD",), ("NDH",), ("P0",))
        ts(T.dum[:], T.dq[:], T.pmf[:, 0:1], None, A.add, None, ("dq", "pmf"), ("dum",))
        ts(T.basec[:], T.pmf[:, 0:1], 2048.0, None, A.add, None, ("pmf",), ("basec",))
        ts(T.nE[:], T.E[:, 0:16], -1.0, 1.0, A.mult, A.add, ("E",), ("nE",))
        ts(T.negE[:], T.E[:, 0:16], -1.0, None, A.mult, None, ("E",), ("negE",))
        cp("v", T.offs[:, 0:1], T.pm[:, 0:1], ("pm",), ("off0",))
        for t in range(4):
            cp("v", T.LT[:, 128 * t + t:128 * t + 128:16], T.BO16[:, t:128:16], ("BO16", "LT"), ("LTx",))
            ts(T.ND[:, 128 * t:128 * t + 128], T.I16[:], T.nE[:, t:t + 1], None, A.mult, None, ("I16", "nE"), ("ND",))
        cp("v", T.TR16[:], T.TRb[:], ("TRb",), ("TR16",))

    def bar_of_own_office(t):
        act(T.DTH[:, 256 * t:256 * t + 256], T.NDH[:], F.Copy, ("NDH",), ("DTH%d" % t,), bias=2.0 ** (6 * (8 + t - 3)))

    def setup_scalar():
        for t in range(4):
            act(T.DT[:, 256 * t:256 * t + 256], T.Dm[:], F.Copy, ("Dm",), ("DT%d" % t,), scale=2.0 ** (6 * (8 + t)))
        for t, n in ((11, "D11"), (12, "D12")):
            act(T[n][:], T.Dm[:], F.Copy, ("Dm",), (n,), scale=float(t))

    for t in range(NR):
        last = t == NR - 1
        cn = "ca" if t % 2 == 0 else "cb"
        C = T[cn]
        c, cprev = C[:, 1:17], C[:, 0:16]
        cu, rcv, scl = T["cu%d" % t], T["rcv%d" % t], T["scl%d" % t]
        cuk, rcvk, sclk = "cu%d" % t, "rcv%d" % t, "scl%d" % t
        p = T.cores[(rank - 1 - t % 5) % 6]
        rep, repk = T["rep%d" % t], "rep%d" % t
        lastw[rcvk] = ("rl%d" % t, 8)
        lastw["rrv%d" % t] = ("rr%d" % t, 8)
        KB = ("P2", "P7")
        eqpos = [256]
        for b in range(15):
            eqpos.append(eqpos[b] + 16 * (15 - b))

        def ask(k):
            a, b = ASK[k]
            cp("v" if k in ASKV else "s", T.Vq[:, 16 * a:16 * b], T.Vw[:, 0:W].indirect(T.kcq[:, a:b]), ("Vw", "kcq"), ("Vq%d" % k,))

        def ask_mm(k):
            a, b = ASK[k]
            for m in range(16):
                mm(T.P1[:, a:b], T.Ib[:], T.Vq[:, 16 * a + m:16 * b:16], m == 0, m == 15, ("Ib", "Vq%d" % k), ("pA%d" % k,), ("P1",))

        def own(k):
            a, b = OWN[k]
            cp("s", T.Vg[:, 16 * a:16 * b], T.Vw[:, 0:W].indirect(T.kc[:, a:b]), ("Vw", "kc"), ("Vg%d" % k,))

        def own_mm(k):
            a, b = OWN[k]
            for m in range(16):
                mm(T.P0[:, a:b], T.Ib[:], T.Vg[:, 16 * a + m:16 * b:16], False, False, ("Ib", "Vg%d" % k), ("pS",), ("P0",))

        def wealth(h):
            tt(T.Dx[:, 2048 * h:2048 * h + 2048], T.Xw[:].indirect(T.kc[:, 128 * h:128 * h + 128]), T.XCr[:, 2048 * h:2048 * h + 2048],
               A.max, ("Xw", "kc") + tuple("XCr%d" % m for m in range(16)), ("Dx%d" % h,))

        def key(h, m=None):
            if m is None:
                return T.P2[:, 0:128] if h == 0 else T.P7[:, 0:128]
            return T.P2[:, m:128:16] if h == 0 else T.P7[:, m:128:16]

        def score_mm(h):
            mm(key(h), T.Ib[:], T.Cm[:, 128 * h:128 * h + 128], True, False, ("Ib", "Cm"), ("pKey%d" % h,), (KB[h],))
            for m in range(16):
                mm(key(h, m), T.Dx[:, 2048 * h + m:2048 * h + 2048:16], T.Gs[:], False, m == 15,
                   ("Dx%d" % h, "Gs"), ("pKey%d" % h,), (KB[h],))

        def eq_v():
            for b in range(15):
                ts(T.EQ[:, eqpos[b]:eqpos[b + 1]], T.crow[:, 16 * b + 16:256], T.c1[:, b:b + 1], None, A.is_equal, None, ("crow", "c1"), ("EQ%d" % b,))

        def eq_mm():
            for b in range(15):
                mm(T.P5[:, 16 * b + 16:256], T.BOb[:], T.EQ[:, eqpos[b]:eqpos[b + 1]], False, b == 14, ("BOb", "EQ%d" % b), ("pcnt",), ("P5",))

        def best_a(h):
            a, b = 128 * h, 128 * h + 128
            scan(T.y[:, a:b], T.seg[:, 0:128], key(h), A.mult, A.max, ("seg", "pKey%d" % h), ("y%d" % h,), (KB[h],))
            tt(T.eqn[:, a:b], key(h), T.y[:, a:b], A.is_equal, ("pKey%d" % h, "y%d" % h), ("eqn%d" % h,), (KB[h],))
            tt(T.neq[:, a:b], key(h), T.y[:, a:b], A.not_equal, ("pKey%d" % h, "y%d" % h), ("neq%d" % h,), (KB[h],))

        def best_b(h):
            a, b = 128 * h, 128 * h + 128
            tt(T.ek[:, a:b], T.P3[:, a:b], T.eqn[:, a:b], A.mult, ("pkc", "eqn%d" % h), ("ek%d" % h,), ("P3",))
            scan(T.s2[:, a:b], T.neq[:, a:b], T.ek[:, a:b], A.mult, A.add, ("neq%d" % h, "ek%d" % h), ("s2_%d" % h,))

        def best_c(h):
            a, b = 128 * h, 128 * h + 128
            tt(T.Bx[:, a:b], T.s2[:, a:b].indirect(T.RL2[:, 0:8]), T.E[:, a:b], A.mult, ("s2_%d" % h, "RL2", "E"), ("Bx%d" % h,))

        def best_mm(h):
            mm(T.P4[:, 8 * h:8 * h + 8], T.Bx[:, 128 * h:128 * h + 128], T.G16[:], True, True, ("Bx%d" % h, "G16"), ("pBest",), ("P4",))

        if t == 0:
            setup_vector()
        cp("v", T.kc[:], T.Kw[:, 0:W].indirect(cu[:]), ("Kw", cuk), ("kc",))
        if t > 0:
            tt(T.Vw[:].indirect(T["scl%d" % (t - 1)][:]), T.VC[:], T.DT[:, 256 * (t - 1):256 * t], A.add, ("VC", "DT%d" % (t - 1), "scl%d" % (t - 1)), ("Vw",))
        if last:
            cp("v", T.SL[:].indirect(T.offs[:, 2 * t:2 * t + 1]), T.mk4[:], ("mk4", "off%d" % t, cn, cuk), ("SL",))
            for h in range(2):
                cp("v", T.SLd[:, 256 * h:256 * h + 256], T.SL[:], ("SL",), ("SLd%d" % h,))
            for r in range(16):
                x = 16 * ((16 - r) % 16)
                mm(T.P6[:, 256:512], T.Dr[:, 128 * r:128 * r + 128], T.SLd[:, x:x + 256], r == 0, r == 15, ("Dr", "SLd0", "SLd1"), ("pSU",), ("P6",))
        cp("s", T.XC[:], T.Xw[:].indirect(cu[:]), ("Xw", cuk), ("XC",))
        for m in range(NS):
            cp("s", T.XCr[:, m:4096:16], T.XC[:], ("XC",), ("XCr%d" % m,))
        cp("s", T.VC[:], T.Vw[:, 0:W].indirect(cu[:]), ("Vw", cuk), ("VC",))
        ts(T.c1[:], c, 1.0, None, A.add, None, (cn,), ("c1",))
        cp("v", T.kc16[:], T.kc[:], ("kc",), ("kc16",))
        tt(T.cE[:], T.c1[:].indirect(T.RL1[:]), T.E[:], A.mult, ("c1", "RL1", "E"), ("cE",))
        for m in range(NS, 16):
            cp("v", T.XCr[:, m:4096:16], T.XC[:], ("XC",), ("XCr%d" % m,))
        cp("v", T.kcq[:], T.Kw[:, 0:W].indirect(rcv[:]), ("Kw", rcvk), ("kcq",))
        for k in range(PRE):
            own(k)
        for k in ASKO:
            ask(k)
        mm(T.P4[:, 0:256], T.BO16[:], T.cE[:], True, True, ("BO16", "cE"), ("pcrow",), ("P4",))
        mm(T.P4[:, 256:512], T.TR16[:], T.cE[:], True, True, ("TR16", "cE"), ("pcrow",), ("P4",))
        for h in range(2):
            mm(T.P3[:, 128 * h:128 * h + 128], T.kc16[:, 128 * h:128 * h + 128], T.I16[:], True, True, ("kc16", "I16"), ("pkc",), ("P3",))
        if not last:
            mm(T.P3[:, 256:512], T.ND[:, 128 * t:128 * t + 128], T.kc16[:], True, False, ("ND", "kc16"), ("pnK",), ("P3",))
            mm(T.P3[:, 256:512:2], T.LT[:, 128 * t:128 * t + 128], T.cE[:, 1:256:2], False, False, ("LTx", "cE"), ("pnK",), ("P3",))
            mm(T.P3[:, 257:512:2], T.LT[:, 128 * t:128 * t + 128], T.cE[:, 0:256:2], False, True, ("LTx", "cE"), ("pnK",), ("P3",))
        if last:
            ts(T.Rw[:, 0:W], T.r24[:], 16.0, None, A.subtract, None, ("r24",), ("Rw",))
            tt(T.nR[:], T.Rw[:, 0:W].indirect(T.cu3[:]), T.D11[:], A.max, ("Rw", "cu3", "D11"), ("nR",))

        mm(T.P0[:, 0:256], T.Ib[:], T.VC[:], True, False, ("Ib", "VC"), ("pS",), ("P0",))
        for k in range(PRE):
            own_mm(k)
        for k in ASKO:
            ask_mm(k)
        for k in range(PRE, MID):
            own(k)
        cp("s", rep[:], T.P1[:, 0:256], tuple("pA%d" % k for k in ASKO), (repk,), ("P1",))
        send(T["rrv%d" % t][:], rep[:], "rr%d" % t, p, (repk,))
        wealth(0)
        cp("v", T.crow[:], T.P4[:], ("pcrow",), ("crow",), ("P4",))
        tt(T.EQ[:, 0:256], T.c1[:].indirect(T.RL1[:]), T.crow[:, 256:512], A.is_equal, ("c1", "RL1", "crow"), ("EQin",))
        eq_v()
        score_mm(0)
        if t == 0:
            cp("v", T.SL[:], T.P5[:, 0:256], ("pSL",), ("SL",), ("P5",))
        mm(T.P5[:, 0:256], T.BOb[:], T.EQ[:, 0:256], True, False, ("BOb", "EQin"), ("pcnt",), ("P5",))
        eq_mm()
        for k in range(PRE, MID):
            own_mm(k)
        wealth(1)
        own(MID)
        own_mm(MID)
        score_mm(1)
        for k in range(MID + 1, len(OWN)):
            own(k)
        act(T.UU[:, 512:768], T.P5[:, 0:256], F.Copy, ("pcnt",), ("UUn",), ("P5",), scale=4.0)
        if not last:
            bar_of_own_office(t + 1)
        if t == 0:
            bar_of_own_office(0)
        best_a(0)
        best_b(0)
        best_c(0)
        for k in range(MID + 1, len(OWN)):
            own_mm(k)
        if t == 3:
            act(T.lnb[:], T.Vw[:, 0:W], F.Ln, ("Vw",), ("lnb",), scale=2.0 ** -48)
            act(T.r24[:], T.lnb[:], F.Copy, ("lnb",), ("r24",), scale=1.0 / (6.0 * math.log(2.0)), bias=24.0)
        if last:
            cp("v", T.Rw[:].indirect(T.scl3[:]), T.nR[:], ("nR", "scl3", "Rw"), ("Rw",))
            tt(T.nR[:], T.Rw[:, 0:W].indirect(cu[:]), T.D12[:], A.max, ("Rw", cuk, "D12"), ("nR",))
            ts(T.msk[:], T.P6[:, 256:512], 4096.0, None, A.is_ge, None, ("pSU",), ("msk",), ("P6",))
            ts(T.ltm[:], T.P6[:, 256:512], 4096.0, None, A.is_lt, None, ("pSU",), ("ltm",), ("P6",))
            tt(T.SLz[:], T.P6[:, 256:512], T.ltm[:], A.mult, ("pSU", "ltm"), ("SLz",), ("P6",))
        best_a(1)
        mm(T.P0[:, 0:256], T.Ib[:], T["rrv%d" % t][:], False, True, ("Ib", "rrv%d" % t), ("pS",), ("P0",))
        ts(T.UU[:, 0:256], T.P0[:, 0:256], 2.0 ** (6 * (8 + t - 2)), None, A.is_ge, None, ("pS",), ("UU2",), ("P0",))
        tt(T.UU[:, 256:512], T.P0[:, 0:256], T.DTH[:, 256 * t:256 * t + 256], A.is_ge, ("pS", "DTH%d" % t), ("UU3",), ("P0",))
        for j in range(16):
            mm(T.P6[:, 0:48], T.Zw[:, 15 - j:143 - j], T.UU[:, j:768:16], j == 0, j == 15, ("Zw", "UU2", "UU3", "UUn"), ("pF",), ("P6",))
        best_b(1)
        if not last:
            act(T.nK[:], T.P3[:, 256:512], F.Identity, ("pnK", "negE"), ("nK",), ("P3",), bias=T.negE[:, t:t + 1])
        if t == 0:
            setup_scalar()
        best_c(1)
        best_mm(0)
        best_mm(1)
        cp("v", T.Bf[:], T.P6[:, 0:48], ("pF",), ("Bf",), ("P6",))
        sm = [T.sm[:, 16 * k:16 * k + 16] for k in range(16)]
        tt(T.wi[:], T.Bf[:, 0:16], T.Bf[:, 32:48], A.add, ("Bf",), ("wi",))
        ts(sm[0], T.Bf[:, 16:32], 8.0, None, A.mult, None, ("Bf",), ("d8",))
        tt(T.gq[:], T.wi[:], sm[0], A.max, ("wi", "d8"), ("gq",))
        ts(T.pp[:], T.wi[:], 1, None, A.bitwise_and, None, ("wi",), ("pp",))
        ts(sm[1], T.wi[:], 12.0, None, A.is_lt, None, ("wi",), ("lt12",))
        if not last:
            ts(T.nirep[:], T.gq[:].indirect(T.RL3[:, 0:8]), 8.0, None, A.is_ge, None, ("gq", "RL3"), ("nirep",))
            mm(T.P6[:, 64:65], T.nirep[:], T.m16[:, 0:1], True, True, ("nirep", "m16"), ("pOff",), ("P6",))
        ts(sm[2], T.gq[:], 8.0, None, A.is_ge, None, ("gq",), ("ni",))
        ts(sm[3], T.wi[:], 64.0, None, A.is_lt, None, ("wi",), ("lt64",))
        tt(sm[4], T.pp[:], sm[1], A.mult, ("pp", "lt12"), ("m1",))
        tt(sm[6], sm[2], T.dum[:], A.mult, ("ni", "dum"), ("nd",))
        tt(sm[7], sm[3], sm[1], A.subtract, ("lt64", "lt12"), ("tb",))
        tt(sm[5], sm[4], sm[2], A.mult, ("m1", "ni"), ("m2",))
        tt(sm[8], sm[6], c, A.max, ("nd", cn), ("lst",))
        tt(T.NT[:, 0:16], sm[2], sm[7], A.subtract, ("ni", "tb", "NT"), ("NT",))
        cp("v", scl[:], sm[8], ("lst",), (sclk,))
        tt(T.mv[:, 1:17], sm[5], T.NT[:, 1:17], A.is_gt, ("m2", "NT", "mv"), ("mv",))
        if last:
            cp("v", T.Rw[:].indirect(scl[:]), T.nR[:], ("nR", sclk, "Rw"), ("Rw",))
            dma("y", "dout", T.yr[:, :], T.Rw[:, 0:W], r=("Rw",))
        else:
            ts(T.yo[:, 0:1], T.P6[:, 64:65], T.basec[:, 0:1], float(16 * (t + 1)), A.add, A.add, ("pOff", "basec"), ("yo",), ("P6",))
        tt(sm[9], T.NT[:, 0:16], T.mv[:, 1:17], A.is_gt, ("NT", "mv"), ("NM",))
        tt(sm[11], T.mv[:, 0:16], cprev, A.mult, ("mv", cn), ("R2",))
        if not last:
            ts(T.yo[:, 1:2], T.yo[:, 0:1], 255, None, A.bitwise_and, None, ("yo",), ("ya",))
        tt(sm[10], sm[9], c, A.mult, ("NM", cn), ("R1",))
        tt(sm[12], sm[9], T.mv[:, 0:16], A.add, ("NM", "mv"), ("q1",))
        tt(sm[13], sm[10], sm[11], A.add, ("R1", "R2"), ("R12",))
        ts(sm[14], sm[12], -1.0, 1.0, A.mult, A.add, ("q1",), ("Bm",))
        if not last:
            cp("v", T.offs[:, 2 * t + 2:2 * t + 3], T.yo[:, 1:2], ("ya",), ("off%d" % (t + 1),))
        tt(sm[15], T.P4[:, 0:16], sm[14], A.mult, ("pBest", "Bm"), ("xb",), ("P4",))
        tt(T.nw[:], sm[15], sm[13], A.add, ("xb", "R12"), ("nw",))
        if not last:
            cp("v", T.SL[:].indirect(T.offs[:, 2 * t:2 * t + 1]), T.nw[:], ("nw", "off%d" % t, "SL"), ("SL",))
            n = t + 1
            nn = "cb" if t % 2 == 0 else "ca"
            cp("v", T["cu%d" % n][:], T.SL[:].indirect(T.offs[:, 2 * n:2 * n + 1]), ("SL", "off%d" % n), ("cu%d" % n,))
            send(T["rcv%d" % n][:], T["cu%d" % n][:], "rl%d" % n, T.cores[(rank + 1 + n % 5) % 6], ("cu%d" % n,))
            cp("v", T[nn][:, 1:17], T.SL[:].indirect(T.offs[:, 2 * n:2 * n + 1]), ("SL", "off%d" % n, nn), (nn,))
            cp("v", T.Kw[:].indirect(scl[:]), T.nK[:], ("nK", sclk, "Kw"), ("Kw",))
        else:
            tt(T.nm[:], T.nw[:].indirect(T.RL3[:]), T.msk[:], A.mult, ("nw", "RL3", "msk"), ("nm",))
            for h in range(2):
                a, b = 256 + 128 * h, 384 + 128 * h
                mm(T.P4[:, a:b], T.SLz[:, 128 * h:128 * h + 128], T.I16[:], True, False, ("SLz", "I16"), ("pY",), ("P4",))
                mm(T.P4[:, a:b], T.nm[:, 128 * h:128 * h + 128], T.I16[:], False, True, ("nm", "I16"), ("pY",), ("P4",))
            cp("v", T.ysb[:], T.P4[:, 256:512], ("pY",), ("ysb",), ("P4",))
            for k in range(16):
                gg, h = k // 2, k % 2
                dma("y" if h == 0 else "s", "dout", T.ys[16 * gg + 8 * h:16 * gg + 8 * h + 8, :],
                    T.ysb[:, 128 * h + 16 * gg:128 * h + 16 * gg + 16], r=("ysb",))
    for s in ("v", "s", "t", "g", "dsl", "dk", "dr", "dx", "loc", "dout"):
        wait("g", (s, cnt[s]))
    for t in range(NR):
        wait("g", ("rl%d" % t, 8))
        wait("g", ("rr%d" % t, 8))
